import numpy as np, ml_dtypes
CORES = [25,29,65,69,153,157,193,197]
N = 8
BF = ml_dtypes.bfloat16
def gentries(a):
    return np.ascontiguousarray(a.reshape(8, 16, -1).transpose(0, 2, 1)).reshape(8, -1)
def gtable(e):
    e = np.asarray(e); return np.ascontiguousarray(e.reshape(8, -1, 16).transpose(0, 2, 1)).reshape(128, -1).astype(np.int32)
V, G, CAP, D, SH, RO = 1024, 384, 96, 4, 3, 3
def parts(rng):
    t = rng.integers(2 ** 18, 2 ** 19, (N, 8, 16, 1))
    r = np.minimum((t * rng.random((N, 8, 1, V)) * rng.random((N, 8, 16, V))).astype(np.int64), t - 1)
    nb = rng.integers(0, V + (N - 1) * G, (N, 8, D * V)); snd = np.argsort(rng.random((N, 8, N - 1, V)), axis=-1)[..., :G]
    return t, r, nb, np.ascontiguousarray(snd)
def heat(rng, t, r, share):
    m = (rng.random((N, 8, 1, V)) < share) & (rng.random(r.shape) < rng.random((N, 8, 1, V)))
    return np.where(m, np.minimum(t + ((2 ** 20 - t) * rng.random(r.shape)).astype(np.int64), 2 ** 20 - 1), r)
def pack(t, r, nb, snd):
    return {"r0": np.ascontiguousarray(r.reshape(N, 128, V)).astype(np.int32), "th": np.ascontiguousarray(t.reshape(N, 128, 1)).astype(np.int32),
            "nb": np.stack([gtable(a) for a in nb]), "snd": np.stack([gtable(a.reshape(8, -1)) for a in snd])}
def setup_inputs(rng):
    t, r, nb, snd = parts(rng); share = rng.choice(np.array([0.05, 0.15, 0.3, 0.5]), (N, 8, 1, 1))
    return pack(t, heat(rng, t, r, share), nb, snd)
def setup_inputs_room(rng):
    t, r, nb, snd = parts(rng); h = V // 2
    for q in range(N):
        for g in range(8):
            o = rng.permutation(V); a, b = o[:h], o[h:]; i = rng.integers(0, 16, h); lo = t[q, g, i, 0]
            r[q, g, i, a] = np.where(rng.random(h) < 0.5, lo, np.minimum(lo + ((2 ** 20 - lo) * rng.random(h)).astype(np.int64), 2 ** 20 - 1))
            for d in range(N - 1):
                n = int(rng.choice(np.array([0, 1, CAP - 1, CAP, CAP + 1, G])))
                if q == 0 and d == 0: n = (CAP, CAP + 1, G, CAP - 1, 1, 0, CAP, CAP + 1)[g]
                snd[q, g, d] = rng.permutation(np.concatenate([rng.permutation(a)[:n], rng.permutation(b)[:G - n]]))
    return pack(t, r, nb, snd)
def setup_inputs_ties(rng):
    t, r, nb, snd = parts(rng)
    base = rng.choice(np.array([1, 4, 7, 1000, 2 ** 16 - 1, 2 ** 19, 2 ** 20 - 1]), (N, 8, 1, 1)); base[0, 0] = 1; base[0, 1] = 2 ** 19; base[1, 0] = 2 ** 20 - 1
    t = np.minimum(base + rng.integers(0, 3, (N, 8, 16, 1)), 2 ** 20)
    r = (t - 1) * rng.integers(0, 2, (N, 8, 16, V)); hit = rng.random((N, 8, 1, V)) < 0.2
    r = np.where(hit, np.minimum(t - 1 + rng.integers(0, 3, r.shape), 2 ** 20 - 1), r)
    m = rng.permutation(V)[None, :]
    r[0, 0] = np.where(m < 3 * V // 10, t[0, 0], np.where(m < 6 * V // 10, rng.integers(2 ** 19, 2 ** 20, (16, V)), t[0, 0] - 1))
    return pack(t, r, nb, snd)
def setup_inputs_alike(rng):
    t, r, nb, snd = parts(rng); r = heat(rng, t, r, 0.2); r[..., 0] = 2 ** 20 - 1; r[..., V - 1] = 2 ** 20 - 1
    snd[:, ::2] = rng.choice(np.array([0, V - 1, V // 2, 3]), (N, 4, N - 1, G))
    nb[:, 1::2] = np.tile(nb[:, 1::2, :V], (1, 1, D))
    nb[:, 2] = rng.integers(V, V + (N - 1) * G, (N, D * V)); nb[:, 4] = rng.integers(0, V, (N, D * V))
    nb[:, 6] = rng.choice(np.array([0, V - 1, V, V + (N - 1) * G - 1]), (N, D * V))
    return pack(t, r, nb, snd)
def setup_inputs_cold(rng):
    t, r, nb, snd = parts(rng); share = rng.choice(np.array([0.1, 0.25, 0.4]), (N, 8, 1, 1))
    q = rng.permutation(N); share[q[0]] = 1.0; share[q[1]] = 0.0; share[:, rng.integers(0, 8)] = 0.0
    return pack(t, heat(rng, t, r, share), nb, snd)
def setup_inputs_spread(rng):
    t, r, nb, snd = parts(rng)
    t = np.minimum(np.maximum(np.exp2(10 + 10 * rng.random((N, 8, 16, 1))).astype(np.int64), 1), 2 ** 20)
    r = np.minimum((np.exp2(20 * rng.random((N, 8, 1, V))) * rng.random((N, 8, 16, V))).astype(np.int64), 2 ** 20 - 1)
    return pack(t, r, nb, snd)
def check_inputs(d):
    bad = []
    for k, lo, hi in (("r0", 0, 2 ** 20 - 1), ("th", 1, 2 ** 20), ("nb", 0, V + (N - 1) * G - 1), ("snd", 0, V - 1)):
        if np.min(d[k]) < lo or np.max(d[k]) > hi: bad.append("range of " + k)
    return bad
def reference(r0, th, nb, snd):
    r = r0.astype(np.int64).reshape(N, 8, 16, V); t = th.astype(np.int64).reshape(N, 8, 16, 1); p = np.zeros((N, 8, 16, V), np.int64)
    nbl = np.stack([gentries(a) for a in nb]).astype(np.int64); sl = np.stack([gentries(a) for a in snd]).astype(np.int64).reshape(N, 8, N - 1, G)
    for rnd in range(RO):
        over = r >= t; s = np.where(over, r >> SH, 0)
        p = p + np.where(over, r - D * s, 0); r = np.where(over, 0, r)
        hot = np.any(over, axis=2)
        come = []
        for a in range(N):
            w = [s[a]]
            for d in range(1, N):
                q = (a - d) % N; ix = sl[q, :, d - 1]
                h = np.take_along_axis(hot[q], ix, 1).astype(np.int64); before = np.add.accumulate(h, axis=1) - h
                v = np.take_along_axis(s[q], ix[:, None, :], 2)
                w.append(np.where(((h == 1) & (before < CAP))[:, None, :], v, 0))
            w = np.concatenate(w, axis=2)
            come.append(np.add.reduce(np.take_along_axis(w, nbl[a][:, None, :], 2).reshape(8, 16, D, V), axis=2))
        r = r + np.stack(come)
    return {"yp": p.reshape(N, 128, V).astype(np.float32), "yr": r.reshape(N, 128, V).astype(np.float32)}

@@ -1,0 +1,324 @@
+from concourse.mybir import AluOpType as ALU, ActivationFunctionType as ACT
+
+V, G, NB, RO, N = 1024, 384, 4, 3, 8
+SIM_CORES = 256
+WW = V + (N - 1) * G
+PA, PB, PC = (0, 320), (320, 640), (640, 1024)
+NC = PC[1] - PC[0]
+STEP = float(2 ** 19)
+BIG = float(2 ** 23)
+
+SCRATCH = {
+    "W0": ("sbuf", [128, WW], "float32"), "W1": ("sbuf", [128, WW], "float32"), "W2": ("sbuf", [128, WW], "float32"),
+    "X": ("sbuf", [128, (N - 1) * G], "float32"),
+    "ri": ("sbuf", [128, V], "int32"), "rb": ("sbuf", [128, V], "float32"), "rm": ("sbuf", [128, V], "float32"),
+    "si": ("sbuf", [128, V], "int32"), "u": ("sbuf", [128, V], "bfloat16"), "hot": ("sbuf", [128, V], "bfloat16"),
+    "po": ("sbuf", [128, V], "float32"),
+    "Hg": ("sbuf", [128, (N - 1) * G], "bfloat16"), "M": ("sbuf", [128, (N - 1) * G], "bfloat16"),
+    "G2": ("sbuf", [128, NB * NC], "float32"),
+    "thi": ("sbuf", [128, 8], "int32"), "bias": ("sbuf", [128, 8], "float32"), "nbias": ("sbuf", [128, 8], "float32"),
+    "sndi": ("sbuf", [128, 168], "int32"), "snd16": ("sbuf", [128, 168], "uint16"),
+    "nbi": ("sbuf", [128, 256], "int32"), "nb16": ("sbuf", [128, 256], "uint16"),
+    "ones": ("sbuf", [128, 128], "bfloat16"), "BD": ("sbuf", [128, 128], "bfloat16"), "IB": ("sbuf", [128, 128], "bfloat16"),
+    "IF": ("sbuf", [128, 384], "float32"), "zer": ("sbuf", [128, G], "bfloat16"),
+    "P0": ("psum", [128, 512], "float32"), "P1": ("psum", [128, 512], "float32"), "R2": ("psum", [128, 512], "float32"),
+    "HA": ("psum", [128, 512], "float32"), "HB": ("psum", [128, 512], "float32"), "HC": ("psum", [128, 512], "float32"),
+    "UA": ("psum", [128, 512], "float32"), "UB": ("psum", [128, 512], "float32"),
+}
+NCS, NDS = 70, 14
+SEMAPHORES = (["c%d" % i for i in range(NCS)] + ["d%d" % i for i in range(NDS)]
+              + ["arr%d" % t for t in range(RO)] + ["snt%d" % t for t in range(RO)]
+              + ["hop%d" % t for t in range(RO)] + ["fwd"])
+
+
+def routes(T, topo):
+    cores = list(T.cores)
+    out = {}
+    for r, src in enumerate(cores):
+        sib, direct, near, far = [], [], [], []
+        for d in range(1, N):
+            dst = cores[(r + d) % N]
+            if dst in topo.cores_of(src):
+                sib.append((d, dst, None))
+            elif topo.may_write(src, dst):
+                direct.append((d, dst, None))
+            elif topo.host(dst) == topo.host(src):
+                hs = [h for h in topo.cores_of(src)
+                      if h not in cores and topo.may_write(h, dst) and topo.die(h) == topo.die(src)]
+                near.append((d, dst, hs[len(near)]))
+            else:
+                hs = [h for h in range(SIM_CORES)
+                      if topo.mates(h, dst) and topo.may_write(h, dst) and topo.may_write(src, h)
+                      and topo.die(h) == topo.die(src)]
+                far.append((d, dst, hs[len(far)]))
+        out[src] = [far[0], near[0], far[1], near[1]] + direct + sib
+    return out
+
+
+def bits(m):
+    return bin(m).count("1")
+
+
+def first_mask(topo, src, to, off):
+    return topo.mask(src, to) & ~off if to in topo.cores_of(src) else topo.mask(src, to)
+
+
+def emit(ops, queues, T):
+    n = len(ops)
+    known = {q: set() for q in queues}
+    closure, deps, before = [None] * n, [None] * n, [None] * n
+    for i, o in enumerate(ops):
+        q = o["q"]
+        need = []
+        for j in range(i - 1, -1, -1):
+            p = ops[j]
+            if j in known[q] or p["remote"]:
+                continue
+            hit = False
+            for (b, lo, hi, w) in o["acc"]:
+                for (b2, lo2, hi2, w2) in p["acc"]:
+                    if b != b2:
+                        continue
+                    if SCRATCH[b][0] == "psum":
+                        if o["grp"] is not None and o["grp"] == p["grp"]:
+                            continue
+                        if w or w2 or q != p["q"]:
+                            hit = True
+                    elif (w or w2) and lo < hi2 and lo2 < hi:
+                        hit = True
+            if hit:
+                need.append(j)
+                known[q] |= closure[j]
+        deps[i] = need
+        before[i] = set(known[q])
+        closure[i] = before[i] | {i}
+    waited = set(j for d in deps for j in d) | set(i for i in range(n) if ops[i]["final"])
+    last = {}
+    ev = {}
+    for i, o in enumerate(ops):
+        eng = queues[o["q"]]
+        for j in deps[i]:
+            eng.wait_ge(T.sem[ev[j][0]], ev[j][1])
+        for (s, c) in o["pre"]:
+            eng.wait_ge(T.sem[s], c)
+        ins = o["fn"]()
+        if i in waited:
+            pool = ["d%d" % k for k in range(NDS)] if o["dma"] else ["c%d" % k for k in range(NCS)]
+            s = [x for x in pool if x not in last or last[x][0] in before[i]][0]
+            step = 16 if o["dma"] else 1
+            c = (last[s][1] if s in last else 0) + step
+            last[s] = (i, c)
+            ev[i] = (s, c)
+            ins.then_inc(T.sem[s], step)
+    for i, o in enumerate(ops):
+        if o["final"]:
+            queues[o["q"]].wait_ge(T.sem[ev[i][0]], ev[i][1])
+
+
+def helper_program(g, core, T, topo, d, dst):
+    rid, pid = topo.addr(dst, core)
+    m = topo.mask(core, dst)
+    lo = V + (d - 1) * G
+    for t in range(RO):
+        blk = T["W%d" % t][:, lo:lo + G]
+        g.wait_ge(T.sem["hop%d" % t], bits(m))
+        g.remote_dma(blk, blk, T.sem["arr%d" % t], T.sem.fwd, pid, rid, m)
+    g.wait_ge(T.sem.fwd, RO * bits(m))
+
+
+def rank_program(g, core, T, topo):
+    plan = routes(T, topo)
+    if T.rank_of(core) is None:
+        for src in plan:
+            for (d, dst, h) in plan[src]:
+                if h == core:
+                    helper_program(g, core, T, topo, d, dst)
+        return
+    mine = plan[core]
+    off = topo.mask(core, mine[0][2])
+    ne = bits(off)
+    v, s_, pe = g.vector, g.scalar, g.tensor
+    queues = {"g": g, "v": v, "s": s_, "pe": pe, "y": g.sync}
+    ops = []
+
+    def op(q, fn, reads, writes, grp=None, pre=(), dma=False, final=False, remote=False):
+        acc = [(b, lo, hi, False) for (b, lo, hi) in reads] + [(b, lo, hi, True) for (b, lo, hi) in writes]
+        ops.append({"q": q, "fn": fn, "acc": acc, "grp": grp, "pre": list(pre), "dma": dma, "final": final,
+                    "remote": remote})
+
+    def ap(x):
+        return T[x[0]][:, x[1]:x[2]]
+
+    def load(q, dst, src):
+        op(q, lambda: queues[q].dma_start(ap(dst), src), [], [dst], dma=True)
+
+    def store(dst, src):
+        op("y", lambda: g.sync.dma_start(dst, ap(src)), [src], [], dma=True, final=True)
+
+    def copy(out, in_):
+        op("v", lambda: v.tensor_copy(ap(out), ap(in_)), [in_], [out])
+
+    def fill(out, c):
+        op("v", lambda: v.memset(ap(out), c), [], [out])
+
+    def ts(out, in_, a, b, o0, o1):
+        op("v", lambda: v.tensor_scalar(ap(out), ap(in_), a, b, o0, o1), [in_], [out])
+
+    def tt(out, a, b, o):
+        op("v", lambda: v.tensor_tensor(ap(out), ap(a), ap(b), o), [a, b], [out])
+
+    def gtt(out, win, lst, b, o, pre=()):
+        op("v", lambda: v.tensor_tensor(ap(out), ap(win).indirect(ap(lst)), ap(b), o), [win, lst, b], [out], pre=pre)
+
+    def act(out, in_, f, scale=1.0, bias=None):
+        if bias is None:
+            op("s", lambda: s_.activation(ap(out), ap(in_), f, scale=scale), [in_], [out])
+        else:
+            op("s", lambda: s_.activation(ap(out), ap(in_), f, bias=ap(bias), scale=scale), [in_, bias], [out])
+
+    def gact(out, win, lst, scale=1.0, pre=()):
+        op("s", lambda: s_.activation(ap(out), ap(win).indirect(ap(lst)), ACT.Copy, scale=scale), [win, lst], [out], pre=pre)
+
+    def mm(out, w, x, start, stop, grp=None):
+        op("pe", lambda: pe.matmul(ap(out), ap(w), ap(x), start, stop), [w, x], [out], grp=grp)
+
+    def sel(out, in_, pat, cmp, base, cm):
+        op("g", lambda: g.affine_select(ap(out), ap(in_), pat, cmp, 0.0, base, cm), [in_], [out])
+
+    def at(b, p):
+        return (b, p[0], p[1])
+
+    def bank(b, p):
+        return (b, 0, p[1] - p[0])
+
+    BD, IB = ("BD", 0, 128), ("IB", 0, 128)
+    I1, IM, I4 = ("IF", 0, 128), ("IF", 128, 256), ("IF", 256, 384)
+    bias, nbias = ("bias", 0, 1), ("nbias", 0, 1)
+    H0, H1 = (0, 512), (512, 1024)
+
+    load("y", at("ri", PA), T.r0[:, PA[0]:PA[1]])
+    load("s", ("thi", 0, 1), T.th[:])
+    load("s", at("ri", PB), T.r0[:, PB[0]:PB[1]])
+    load("y", at("ri", PC), T.r0[:, PC[0]:PC[1]])
+    load("s", ("sndi", 0, 168), T.snd[:])
+    load("y", ("nbi", 0, 256), T.nb[:])
+    fill(("ones", 0, 128), 1.0)
+    fill(I1, 1.0)
+    fill(IM, -1.0)
+    fill(I4, -4.0)
+    fill(("zer", 0, G), 0.0)
+    sel(BD, ("ones", 0, 128), [[-16, 8], [0, 16]], ALU.is_ge, 0, 1)
+    sel(IB, ("ones", 0, 128), [[-1, 128]], ALU.is_equal, 0, 1)
+    sel(BD, BD, [[16, 8], [0, 16]], ALU.is_ge, 15, -1)
+    sel(("IF", 0, 384), ("IF", 0, 384), [[0, 3], [-1, 128]], ALU.is_equal, 0, 1)
+    ts(bias, ("thi", 0, 1), -BIG, BIG / 2, ALU.mult, ALU.add)
+    copy(at("rb", PA), at("ri", PA))
+
+    def mk_u(p, src):
+        act(at("u", p), src, ACT.Relu, BIG, bias)
+
+    def mk_s(p):
+        ts(at("si", p), at("rm", p), 0.125, -0.4375, ALU.mult, ALU.add)
+
+    def mk_hot(p, h):
+        act(at("hot", p), bank(h, p), ACT.Sign)
+
+    def mk_rm(p, ub):
+        tt(at("rm", p), at("rb", p), bank(ub, p), ALU.min)
+
+    for t in range(RO):
+        W = "W%d" % t
+        if t == 0:
+            mk_u(PA, at("rb", PA)); mm(bank("HA", PA), BD, at("u", PA), True, True); mm(bank("UA", PA), IB, at("u", PA), True, True)
+            copy(at("rb", PB), at("ri", PB))
+            mk_u(PB, at("rb", PB)); mm(bank("HB", PB), BD, at("u", PB), True, True); mm(bank("UB", PB), IB, at("u", PB), True, True)
+            copy(at("rb", PC), at("ri", PC))
+            mk_hot(PA, "HA")
+            mk_u(PC, at("rb", PC)); mm(bank("HC", PC), BD, at("u", PC), True, True); mm(bank("R2", PC), IB, at("u", PC), True, True)
+            copy(("snd16", 0, 168), ("sndi", 0, 168))
+            mk_hot(PB, "HB"); mk_hot(PC, "HC")
+            mk_rm(PA, "UA"); mk_rm(PB, "UB"); mk_s(PA); mk_rm(PC, "R2"); mk_s(PB); mk_s(PC)
+        else:
+            mk_u(PC, bank("R2", PC)); mm(bank("HC", PC), BD, at("u", PC), True, True)
+            mk_u(PA, at("rb", PA)); mm(bank("UA", PA), IB, at("u", PA), True, True); mm(bank("HA", PA), BD, at("u", PA), True, True)
+            tt(at("rm", PC), bank("R2", PC), at("u", PC), ALU.min)
+            mk_u(PB, at("rb", PB)); mm(bank("UB", PB), IB, at("u", PB), True, True); mm(bank("HB", PB), BD, at("u", PB), True, True)
+            mk_rm(PA, "UA"); mk_s(PC); mk_hot(PC, "HC")
+            mk_rm(PB, "UB"); mk_s(PA); mk_hot(PA, "HA")
+            mk_s(PB); mk_hot(PB, "HB")
+
+        def hot_gather(j):
+            gact(("Hg", j * G, (j + 1) * G), ("hot", 0, V), ("snd16", (mine[j][0] - 1) * 24, mine[j][0] * 24), -STEP)
+
+        def scan(j):
+            m_, h_ = ("M", j * G, (j + 1) * G), ("Hg", j * G, (j + 1) * G)
+            op("v", lambda: v.tensor_tensor_scan(ap(m_), ap(h_), T.zer[:, 0:G], 97.0 * STEP, ALU.add, ALU.max),
+               [h_, ("zer", 0, G)], [m_])
+
+        def send(j, t=t, W=W):
+            d, dst, h = mine[j]
+            x = ("X", j * G, (j + 1) * G)
+            pre = [("snt%d" % (t - 1), (N - 1) * ne)] if (j == 0 and t > 0) else []
+            gtt(x, ("si", 0, V), ("snd16", (d - 1) * 24, d * 24), ("M", j * G, (j + 1) * G), ALU.min, pre=pre)
+            to = dst if h is None else h
+            rid, pid = topo.addr(to, core)
+            m = first_mask(topo, core, to, off)
+            lo = V + (d - 1) * G
+            rs = T.sem[("arr%d" if h is None else "hop%d") % t]
+            op("g", lambda: g.remote_dma(T[W][:, lo:lo + G], ap(x), rs, T.sem["snt%d" % t], pid, rid, m),
+               [x], [], remote=True)
+
+        for j in range(N - 1):
+            hot_gather(j)
+        mm(bank("P0", H0), I1, at("rm", H0), t == 0, False, "p0")
+        mm(bank("P1", H1), I1, at("rm", H1), t == 0, False, "p1")
+        if t > 0:
+            mm(bank("P0", H0), I4, at("W%d" % (t - 1), H0), False, False, "p0")
+            mm(bank("P1", H1), I4, at("W%d" % (t - 1), H1), False, False, "p1")
+        if t == 0:
+            ts(nbias, ("thi", 0, 1), BIG, -BIG / 2, ALU.mult, ALU.add)
+        scan(0); send(0); scan(1); send(1); scan(2)
+        for j in range(2, N - 1):
+            if j + 1 < N - 1:
+                scan(j + 1)
+            send(j)
+        if t > 0:
+            act(at("rb", PC), bank("R2", PC), ACT.Copy)
+        act(bank("UA", PA), at("rb", PA), ACT.Relu, -BIG, nbias)
+        act(bank("UB", PB), at("rb", PB), ACT.Relu, -BIG, nbias)
+        grp = "r%d" % t
+        mm(bank("R2", PC), I1, at("rb", PC), True, False, grp)
+        mm(bank("R2", PC), IM, at("rm", PC), False, False, grp)
+        copy((W, 0, V), ("si", 0, V))
+        if t == RO - 1:
+            mm(bank("P0", H0), I4, at(W, H0), False, True, "p0")
+            mm(bank("P1", H1), I4, at(W, H1), False, True, "p1")
+        tt(at("rb", PA), at("rb", PA), bank("UA", PA), ALU.min)
+        tt(at("rb", PB), at("rb", PB), bank("UB", PB), ALU.min)
+        if t == 0:
+            copy(("nb16", 0, 256), ("nbi", 0, 256))
+
+        arr = [("arr%d" % t, (N - 1) * ne)]
+
+        def lst(i, p):
+            return ("nb16", (i * V + p[0]) // 16, (i * V + p[1]) // 16)
+
+        for i in range(NB):
+            gi = ("G2", i * NC, (i + 1) * NC)
+            gact(gi, (W, 0, WW), lst(i, PC), pre=arr if i == 0 else ())
+            mm(bank("R2", PC), I1, gi, False, i == NB - 1, grp)
+            gtt(at("rb", PA), (W, 0, WW), lst(i, PA), at("rb", PA), ALU.add, pre=arr if i == 0 else ())
+            if t == RO - 1 and i == NB - 1:
+                act(at("po", H0), bank("P0", H0), ACT.Copy)
+                store(T.yp[:, H0[0]:H0[1]], at("po", H0))
+                act(at("po", H1), bank("P1", H1), ACT.Copy)
+                store(T.yp[:, H1[0]:H1[1]], at("po", H1))
+                act(at("rb", PC), bank("R2", PC), ACT.Copy)
+                store(T.yr[:, PA[0]:PA[1]], at("rb", PA))
+                store(T.yr[:, PC[0]:PC[1]], at("rb", PC))
+            gtt(at("rb", PB), (W, 0, WW), lst(i, PB), at("rb", PB), ALU.add)
+        if t == RO - 1:
+            store(T.yr[:, PB[0]:PB[1]], at("rb", PB))
+
+    emit(ops, queues, T)
+    g.wait_ge(T.sem["snt%d" % (RO - 1)], (N - 1) * ne)

@@ -3,8 +3,8 @@ from concourse.mybir import AluOpType as ALU, ActivationFunctionType as ACT
 V, G, NB, RO, N = 1024, 384, 4, 3, 8
 SIM_CORES = 256
 WW = V + (N - 1) * G
-PA, PB, PC = (0, 320), (320, 640), (640, 1024)
-NC = PC[1] - PC[0]
+PA, PB, PC, PD = (0, 288), (288, 576), (576, 800), (800, 1024)
+NC = PD[1] - PC[0]
 STEP = float(2 ** 19)
 BIG = float(2 ** 23)
 
@@ -12,46 +12,57 @@ SCRATCH = {
     "W0": ("sbuf", [128, WW], "float32"), "W1": ("sbuf", [128, WW], "float32"), "W2": ("sbuf", [128, WW], "float32"),
     "X": ("sbuf", [128, (N - 1) * G], "float32"),
     "ri": ("sbuf", [128, V], "int32"), "rb": ("sbuf", [128, V], "float32"), "rm": ("sbuf", [128, V], "float32"),
+    "rho": ("sbuf", [128, V], "float32"), "dif": ("sbuf", [128, V], "float32"),
     "si": ("sbuf", [128, V], "int32"), "u": ("sbuf", [128, V], "bfloat16"), "hot": ("sbuf", [128, V], "bfloat16"),
     "po": ("sbuf", [128, V], "float32"),
     "Hg": ("sbuf", [128, (N - 1) * G], "bfloat16"), "M": ("sbuf", [128, (N - 1) * G], "bfloat16"),
     "G2": ("sbuf", [128, NB * NC], "float32"),
-    "thi": ("sbuf", [128, 8], "int32"), "bias": ("sbuf", [128, 8], "float32"), "nbias": ("sbuf", [128, 8], "float32"),
+    "thi": ("sbuf", [128, 8], "int32"), "col": ("sbuf", [128, 48], "float32"),
     "sndi": ("sbuf", [128, 168], "int32"), "snd16": ("sbuf", [128, 168], "uint16"),
     "nbi": ("sbuf", [128, 256], "int32"), "nb16": ("sbuf", [128, 256], "uint16"),
     "ones": ("sbuf", [128, 128], "bfloat16"), "BD": ("sbuf", [128, 128], "bfloat16"), "IB": ("sbuf", [128, 128], "bfloat16"),
-    "IF": ("sbuf", [128, 384], "float32"), "zer": ("sbuf", [128, G], "bfloat16"),
-    "P0": ("psum", [128, 512], "float32"), "P1": ("psum", [128, 512], "float32"), "R2": ("psum", [128, 512], "float32"),
-    "HA": ("psum", [128, 512], "float32"), "HB": ("psum", [128, 512], "float32"), "HC": ("psum", [128, 512], "float32"),
+    "IF": ("sbuf", [128, 1024], "float32"), "zer": ("sbuf", [128, G], "bfloat16"),
+    "P0": ("psum", [128, 512], "float32"), "P1": ("psum", [128, 512], "float32"),
+    "RC": ("psum", [128, 512], "float32"), "RD": ("psum", [128, 512], "float32"),
+    "H1": ("psum", [128, 512], "float32"), "H2": ("psum", [128, 512], "float32"),
     "UA": ("psum", [128, 512], "float32"), "UB": ("psum", [128, 512], "float32"),
 }
-NCS, NDS = 70, 14
+NCS, NDS = 90, 14
 SEMAPHORES = (["c%d" % i for i in range(NCS)] + ["d%d" % i for i in range(NDS)]
               + ["arr%d" % t for t in range(RO)] + ["snt%d" % t for t in range(RO)]
-              + ["hop%d" % t for t in range(RO)] + ["fwd"])
+              + ["hop%d_%d" % (j, t) for j in range(6) for t in range(RO)] + ["fwd"])
+HG = G // 2
+PLAN = {}
+A, B, AB = (0, HG), (HG, G), (0, G)
+ORDER = [("near", 0, A, "m0"), ("near", 0, B, "o0"), ("far", 0, A, "m1"), ("far", 0, B, "o1"), ("far", 1, A, "m0"),
+         ("far", 1, B, "o0"), ("near", 1, A, "m1"), ("dir", 0, A, "f0"), ("near", 1, B, "m0"), ("dir", 0, B, "o1"),
+         ("dir", 1, AB, ""), ("sib", 0, AB, "")]
 
 
 def routes(T, topo):
     cores = list(T.cores)
     out = {}
-    for r, src in enumerate(cores):
-        sib, direct, near, far = [], [], [], []
+    for src in cores:
+        to = {"sib": [], "dir": [], "near": [], "far": []}
         for d in range(1, N):
-            dst = cores[(r + d) % N]
-            if dst in topo.cores_of(src):
-                sib.append((d, dst, None))
-            elif topo.may_write(src, dst):
-                direct.append((d, dst, None))
-            elif topo.host(dst) == topo.host(src):
-                hs = [h for h in topo.cores_of(src)
-                      if h not in cores and topo.may_write(h, dst) and topo.die(h) == topo.die(src)]
-                near.append((d, dst, hs[len(near)]))
-            else:
-                hs = [h for h in range(SIM_CORES)
-                      if topo.mates(h, dst) and topo.may_write(h, dst) and topo.may_write(src, h)
-                      and topo.die(h) == topo.die(src)]
-                far.append((d, dst, hs[len(far)]))
-        out[src] = [far[0], near[0], far[1], near[1]] + direct + sib
+            dst = cores[(cores.index(src) + d) % N]
+            kind = ("sib" if dst in topo.cores_of(src) else "dir" if topo.may_write(src, dst)
+                    else "near" if topo.host(dst) == topo.host(src) else "far")
+            to[kind].append((topo.die(dst) == topo.die(src), d, dst))
+        other = to["near"][0][2]
+        own = [h for h in topo.cores_of(src) if topo.may_write(h, other) and topo.die(h) == topo.die(src)]
+        free = [h for h in topo.cores_of(src) if h not in own and h != src and topo.die(h) == topo.die(src)]
+        leave = topo.mask(src, to["dir"][0][2])
+        out[src] = []
+        for kind, k, (lo, hi), way in ORDER:
+            _, d, dst = sorted(to[kind])[k]
+            mate = [h for h in range(SIM_CORES) if topo.mates(h, dst) and topo.may_write(h, dst)
+                    and topo.die(h) == topo.die(src)]
+            stops = [src] + [{"o": own, "m": mate, "f": free}[w[0]][int(w[1])] for w in way.split()] + [dst]
+            hops = [(a, b, topo.mask(a, b)) for a, b in zip(stops, stops[1:])]
+            if stops[1] in topo.cores_of(src):
+                hops[0] = (src, stops[1], hops[0][2] & ~leave)
+            out[src].append((d, lo, hi, hops))
     return out
 
 
@@ -59,8 +70,16 @@ def bits(m):
     return bin(m).count("1")
 
 
-def first_mask(topo, src, to, off):
-    return topo.mask(src, to) & ~off if to in topo.cores_of(src) else topo.mask(src, to)
+def relay_jobs(plan, core):
+    return sorted((i, k, d, lo, hi, hops) for src in plan for i, (d, lo, hi, hops) in enumerate(plan[src])
+                  for k in range(1, len(hops)) if hops[k][0] == core)
+
+
+def landing(plan, hops, k, t):
+    if k == len(hops) - 1:
+        return "arr%d" % t
+    slot = [x[5] is hops for x in relay_jobs(plan, hops[k][1])].index(True)
+    return "hop%d_%d" % (slot, t)
 
 
 def emit(ops, queues, T):
@@ -115,28 +134,39 @@ def emit(ops, queues, T):
             queues[o["q"]].wait_ge(T.sem[ev[i][0]], ev[i][1])
 
 
-def helper_program(g, core, T, topo, d, dst):
-    rid, pid = topo.addr(dst, core)
-    m = topo.mask(core, dst)
-    lo = V + (d - 1) * G
+def helper_program(g, core, T, topo, plan, jobs):
+    sent = 0
     for t in range(RO):
-        blk = T["W%d" % t][:, lo:lo + G]
-        g.wait_ge(T.sem["hop%d" % t], bits(m))
-        g.remote_dma(blk, blk, T.sem["arr%d" % t], T.sem.fwd, pid, rid, m)
-    g.wait_ge(T.sem.fwd, RO * bits(m))
+        for slot, (i, k, d, lo, hi, hops) in enumerate(jobs):
+            rid, pid = topo.addr(hops[k][1], core)
+            blk = T["W%d" % t][:, V + (d - 1) * G + lo:V + (d - 1) * G + hi]
+            g.wait_ge(T.sem["hop%d_%d" % (slot, t)], bits(hops[k - 1][2]))
+            g.remote_dma(blk, blk, T.sem[landing(plan, hops, k, t)], T.sem.fwd, pid, rid, hops[k][2])
+            sent += bits(hops[k][2])
+    g.wait_ge(T.sem.fwd, sent)
 
 
 def rank_program(g, core, T, topo):
-    plan = routes(T, topo)
+    if not PLAN:
+        PLAN.update(routes(T, topo))
+    plan = PLAN
     if T.rank_of(core) is None:
-        for src in plan:
-            for (d, dst, h) in plan[src]:
-                if h == core:
-                    helper_program(g, core, T, topo, d, dst)
+        jobs = relay_jobs(plan, core)
+        if jobs:
+            helper_program(g, core, T, topo, plan, jobs)
         return
     mine = plan[core]
-    off = topo.mask(core, mine[0][2])
-    ne = bits(off)
+    n_out = sum(bits(hops[0][2]) for d, lo, hi, hops in mine)
+    n_in = sum(bits(hops[-1][2]) for src in plan for d, lo, hi, hops in plan[src] if hops[-1][1] == core)
+    parts = []
+    for d, lo, hi, hops in mine:
+        part = (d, lo, hi) if d == mine[0][0] else (d, 0, G)
+        if part not in parts:
+            parts.append(part)
+
+    def need(piece):
+        return [k for k, (d, lo, hi) in enumerate(parts) if d == piece[0] and lo <= piece[1] < hi][0]
+
     v, s_, pe = g.vector, g.scalar, g.tensor
     queues = {"g": g, "v": v, "s": s_, "pe": pe, "y": g.sync}
     ops = []
@@ -152,8 +182,8 @@ def rank_program(g, core, T, topo):
     def load(q, dst, src):
         op(q, lambda: queues[q].dma_start(ap(dst), src), [], [dst], dma=True)
 
-    def store(dst, src):
-        op("y", lambda: g.sync.dma_start(dst, ap(src)), [src], [], dma=True, final=True)
+    def store(q, dst, src):
+        op(q, lambda: queues[q].dma_start(dst, ap(src)), [src], [], dma=True, final=True)
 
     def copy(out, in_):
         op("v", lambda: v.tensor_copy(ap(out), ap(in_)), [in_], [out])
@@ -161,8 +191,8 @@ def rank_program(g, core, T, topo):
     def fill(out, c):
         op("v", lambda: v.memset(ap(out), c), [], [out])
 
-    def ts(out, in_, a, b, o0, o1):
-        op("v", lambda: v.tensor_scalar(ap(out), ap(in_), a, b, o0, o1), [in_], [out])
+    def ts(out, in_, a, b, o0, o1, cols=()):
+        op("v", lambda: v.tensor_scalar(ap(out), ap(in_), a, b, o0, o1), [in_] + list(cols), [out])
 
     def tt(out, a, b, o):
         op("v", lambda: v.tensor_tensor(ap(out), ap(a), ap(b), o), [a, b], [out])
@@ -176,8 +206,13 @@ def rank_program(g, core, T, topo):
         else:
             op("s", lambda: s_.activation(ap(out), ap(in_), f, bias=ap(bias), scale=scale), [in_, bias], [out])
 
-    def gact(out, win, lst, scale=1.0, pre=()):
-        op("s", lambda: s_.activation(ap(out), ap(win).indirect(ap(lst)), ACT.Copy, scale=scale), [win, lst], [out], pre=pre)
+    def gact(out, win, lst, scale=1.0, bias=None, pre=()):
+        if bias is None:
+            op("s", lambda: s_.activation(ap(out), ap(win).indirect(ap(lst)), ACT.Copy, scale=scale),
+               [win, lst], [out], pre=pre)
+        else:
+            op("s", lambda: s_.activation(ap(out), ap(win).indirect(ap(lst)), ACT.Identity, bias=ap(bias), scale=scale),
+               [win, lst, bias], [out], pre=pre)
 
     def mm(out, w, x, start, stop, grp=None):
         op("pe", lambda: pe.matmul(ap(out), ap(w), ap(x), start, stop), [w, x], [out], grp=grp)
@@ -188,137 +223,195 @@ def rank_program(g, core, T, topo):
     def at(b, p):
         return (b, p[0], p[1])
 
-    def bank(b, p):
-        return (b, 0, p[1] - p[0])
+    def bank(b, p, lo=0):
+        return (b, lo, lo + p[1] - p[0])
 
     BD, IB = ("BD", 0, 128), ("IB", 0, 128)
-    I1, IM, I4 = ("IF", 0, 128), ("IF", 128, 256), ("IF", 256, 384)
-    bias, nbias = ("bias", 0, 1), ("nbias", 0, 1)
+    I1, I8, IE, I2, IM2, IQ, IMQ, IM1 = [("IF", 128 * k, 128 * k + 128) for k in range(8)]
+    b_r, nb_r, b_q, nb_q, c716, cm35, c35, c105, thf = [("col", 4 * k, 4 * k + 1) for k in range(9)]
+    th = ("thi", 0, 1)
     H0, H1 = (0, 512), (512, 1024)
+    PCD = (PC[0], PD[1])
+    home = {PA: bank("UA", PA), PB: bank("UB", PB), PC: bank("RC", PC), PD: bank("RD", PD)}
+    hsum = {PC: bank("H1", PC), PA: bank("H1", PA, PC[1] - PC[0]), PD: bank("H2", PD), PB: bank("H2", PB, PD[1] - PD[0])}
 
+    def padd(w, buf, p, start=False, stop=None):
+        for k, h in enumerate((H0, H1)):
+            lo, hi = max(p[0], h[0]), min(p[1], h[1])
+            if lo < hi:
+                mm(("P%d" % k, lo - h[0], hi - h[0]), w, (buf, lo, hi), start, stop == k, "p%d" % k)
+
+    load("s", th, T.th[:])
     load("y", at("ri", PA), T.r0[:, PA[0]:PA[1]])
-    load("s", ("thi", 0, 1), T.th[:])
     load("s", at("ri", PB), T.r0[:, PB[0]:PB[1]])
     load("y", at("ri", PC), T.r0[:, PC[0]:PC[1]])
-    load("s", ("sndi", 0, 168), T.snd[:])
+    load("s", at("ri", PD), T.r0[:, PD[0]:PD[1]])
+    load("y", ("sndi", 0, 168), T.snd[:])
     load("y", ("nbi", 0, 256), T.nb[:])
     fill(("ones", 0, 128), 1.0)
     fill(I1, 1.0)
-    fill(IM, -1.0)
-    fill(I4, -4.0)
     fill(("zer", 0, G), 0.0)
+    for c, x in ((c716, 0.4375), (cm35, -3.5), (c35, 3.5), (c105, 10.5)):
+        fill(c, x)
     sel(BD, ("ones", 0, 128), [[-16, 8], [0, 16]], ALU.is_ge, 0, 1)
     sel(IB, ("ones", 0, 128), [[-1, 128]], ALU.is_equal, 0, 1)
     sel(BD, BD, [[16, 8], [0, 16]], ALU.is_ge, 15, -1)
-    sel(("IF", 0, 384), ("IF", 0, 384), [[0, 3], [-1, 128]], ALU.is_equal, 0, 1)
-    ts(bias, ("thi", 0, 1), -BIG, BIG / 2, ALU.mult, ALU.add)
-    copy(at("rb", PA), at("ri", PA))
+    sel(I1, I1, [[-1, 128]], ALU.is_equal, 0, 1)
+    for w, x in ((I2, 2.0), (IM2, -2.0), (IMQ, -0.25), (IE, 0.125)):
+        act(w, IB, ACT.Copy, x)
+    ts(b_q, th, -BIG, 4 * BIG, ALU.mult, ALU.add)
 
-    def mk_u(p, src):
-        act(at("u", p), src, ACT.Relu, BIG, bias)
+    def mk_u(p, src, unit):
+        act(at("u", p), src, ACT.Relu, unit * BIG, b_r if unit == 1 else b_q)
 
-    def mk_s(p):
+    def mk_h(p):
+        mm(hsum[p], BD, at("u", p), True, True)
+
+    def mk_U(p):
+        mm(home[p], IB, at("u", p), True, True)
+
+    def mk_hot(p):
+        act(at("hot", p), hsum[p], ACT.Sign)
+
+    def mk_rho(p):
+        ts(at("rho", p), at("ri", p), 0.125, -0.4375, ALU.mult, ALU.add)
+
+    def mk_rm(p):
+        tt(at("rm", p), at("rb", p), home[p], ALU.min)
+
+    def s_of_rm(p):
         ts(at("si", p), at("rm", p), 0.125, -0.4375, ALU.mult, ALU.add)
 
-    def mk_hot(p, h):
-        act(at("hot", p), bank(h, p), ACT.Sign)
-
-    def mk_rm(p, ub):
-        tt(at("rm", p), at("rb", p), bank(ub, p), ALU.min)
+    def s_of_rho(p, t):
+        tt(at("si", p), at("rho" if t == 0 else "u", p), home[p], ALU.min)
 
     for t in range(RO):
         W = "W%d" % t
+        last = t == RO - 1
         if t == 0:
-            mk_u(PA, at("rb", PA)); mm(bank("HA", PA), BD, at("u", PA), True, True); mm(bank("UA", PA), IB, at("u", PA), True, True)
-            copy(at("rb", PB), at("ri", PB))
-            mk_u(PB, at("rb", PB)); mm(bank("HB", PB), BD, at("u", PB), True, True); mm(bank("UB", PB), IB, at("u", PB), True, True)
-            copy(at("rb", PC), at("ri", PC))
-            mk_hot(PA, "HA")
-            mk_u(PC, at("rb", PC)); mm(bank("HC", PC), BD, at("u", PC), True, True); mm(bank("R2", PC), IB, at("u", PC), True, True)
+            for p in (PA, PB, PC, PD):
+                mk_rho(p); mk_u(p, at("rho", p), 8)
+                for hb, h in (("H1", H0), ("H2", H1)):
+                    lo, hi = max(p[0], h[0]), min(p[1], h[1])
+                    if lo < hi:
+                        mm((hb, lo - h[0], hi - h[0]), BD, ("u", lo, hi), True, True)
+                mk_U(p)
             copy(("snd16", 0, 168), ("sndi", 0, 168))
-            mk_hot(PB, "HB"); mk_hot(PC, "HC")
-            mk_rm(PA, "UA"); mk_rm(PB, "UB"); mk_s(PA); mk_rm(PC, "R2"); mk_s(PB); mk_s(PC)
+            act(("hot", 0, 512), ("H1", 0, 512), ACT.Sign)
+            act(("hot", 512, V), ("H2", 0, 512), ACT.Sign)
+            for p in (PA, PB, PC, PD):
+                s_of_rho(p, t)
         else:
-            mk_u(PC, bank("R2", PC)); mm(bank("HC", PC), BD, at("u", PC), True, True)
-            mk_u(PA, at("rb", PA)); mm(bank("UA", PA), IB, at("u", PA), True, True); mm(bank("HA", PA), BD, at("u", PA), True, True)
-            tt(at("rm", PC), bank("R2", PC), at("u", PC), ALU.min)
-            mk_u(PB, at("rb", PB)); mm(bank("UB", PB), IB, at("u", PB), True, True); mm(bank("HB", PB), BD, at("u", PB), True, True)
-            mk_rm(PA, "UA"); mk_s(PC); mk_hot(PC, "HC")
-            mk_rm(PB, "UB"); mk_s(PA); mk_hot(PA, "HA")
-            mk_s(PB); mk_hot(PB, "HB")
+            mk_u(PA, at("rb", PA), 1); mk_hot(PC); mk_h(PA); mk_U(PA)
+            ts(at("u", PB), at("rb", PB), ap(thf), BIG, ALU.is_ge, ALU.mult, [thf]); mk_h(PB)
+            mk_u(PD, home[PD], 8); mk_hot(PA); mk_U(PB); mk_h(PD); mk_hot(PB); mk_hot(PD)
+            s_of_rho(PC, t); mk_rm(PA); mk_rm(PB); s_of_rm(PA); s_of_rho(PD, t); s_of_rm(PB)
 
-        def hot_gather(j):
-            gact(("Hg", j * G, (j + 1) * G), ("hot", 0, V), ("snd16", (mine[j][0] - 1) * 24, mine[j][0] * 24), -STEP)
+        def hot_gather(d, lo, hi):
+            j = d - 1
+            gact(("Hg", j * G + lo, j * G + hi), ("hot", 0, V), ("snd16", j * 24 + lo // 16, j * 24 + hi // 16), -STEP)
 
-        def scan(j):
-            m_, h_ = ("M", j * G, (j + 1) * G), ("Hg", j * G, (j + 1) * G)
-            op("v", lambda: v.tensor_tensor_scan(ap(m_), ap(h_), T.zer[:, 0:G], 97.0 * STEP, ALU.add, ALU.max),
-               [h_, ("zer", 0, G)], [m_])
+        def scan(d, lo, hi):
+            j = d - 1
+            m_, h_, z_ = ("M", j * G + lo, j * G + hi), ("Hg", j * G + lo, j * G + hi), ("zer", lo, hi)
+            prev = ("M", j * G + lo - 1, j * G + lo)
+            op("v", lambda: v.tensor_tensor_scan(ap(m_), ap(h_), ap(z_), ap(prev) if lo else 97.0 * STEP,
+                                                 ALU.add, ALU.max), [h_, z_] + ([prev] if lo else []), [m_])
 
-        def send(j, t=t, W=W):
-            d, dst, h = mine[j]
-            x = ("X", j * G, (j + 1) * G)
-            pre = [("snt%d" % (t - 1), (N - 1) * ne)] if (j == 0 and t > 0) else []
-            gtt(x, ("si", 0, V), ("snd16", (d - 1) * 24, d * 24), ("M", j * G, (j + 1) * G), ALU.min, pre=pre)
-            to = dst if h is None else h
-            rid, pid = topo.addr(to, core)
-            m = first_mask(topo, core, to, off)
-            lo = V + (d - 1) * G
-            rs = T.sem[("arr%d" if h is None else "hop%d") % t]
-            op("g", lambda: g.remote_dma(T[W][:, lo:lo + G], ap(x), rs, T.sem["snt%d" % t], pid, rid, m),
+        def send(i, t=t, W=W):
+            d, lo, hi, hops = mine[i]
+            j = d - 1
+            x, w = ("X", j * G + lo, j * G + hi), (W, V + j * G + lo, V + j * G + hi)
+            gtt(x, ("si", 0, V), ("snd16", j * 24 + lo // 16, j * 24 + hi // 16), ("M", j * G + lo, j * G + hi), ALU.min,
+                pre=[("snt%d" % (t - 1), n_out)] if (i == 0 and t > 0) else [])
+            rid, pid = topo.addr(hops[0][1], core)
+            rs = T.sem[landing(plan, hops, 0, t)]
+            op("g", lambda: g.remote_dma(ap(w), ap(x), rs, T.sem["snt%d" % t], pid, rid, hops[0][2]),
                [x], [], remote=True)
 
-        for j in range(N - 1):
-            hot_gather(j)
-        mm(bank("P0", H0), I1, at("rm", H0), t == 0, False, "p0")
-        mm(bank("P1", H1), I1, at("rm", H1), t == 0, False, "p1")
-        if t > 0:
-            mm(bank("P0", H0), I4, at("W%d" % (t - 1), H0), False, False, "p0")
-            mm(bank("P1", H1), I4, at("W%d" % (t - 1), H1), False, False, "p1")
+        for part in parts:
+            hot_gather(*part)
         if t == 0:
-            ts(nbias, ("thi", 0, 1), BIG, -BIG / 2, ALU.mult, ALU.add)
-        scan(0); send(0); scan(1); send(1); scan(2)
-        for j in range(2, N - 1):
-            if j + 1 < N - 1:
-                scan(j + 1)
-            send(j)
-        if t > 0:
-            act(at("rb", PC), bank("R2", PC), ACT.Copy)
-        act(bank("UA", PA), at("rb", PA), ACT.Relu, -BIG, nbias)
-        act(bank("UB", PB), at("rb", PB), ACT.Relu, -BIG, nbias)
-        grp = "r%d" % t
-        mm(bank("R2", PC), I1, at("rb", PC), True, False, grp)
-        mm(bank("R2", PC), IM, at("rm", PC), False, False, grp)
-        copy((W, 0, V), ("si", 0, V))
-        if t == RO - 1:
-            mm(bank("P0", H0), I4, at(W, H0), False, True, "p0")
-            mm(bank("P1", H1), I4, at(W, H1), False, True, "p1")
-        tt(at("rb", PA), at("rb", PA), bank("UA", PA), ALU.min)
-        tt(at("rb", PB), at("rb", PB), bank("UB", PB), ALU.min)
-        if t == 0:
-            copy(("nb16", 0, 256), ("nbi", 0, 256))
+            padd(I2, "rho", (0, V), start=True)
+        else:
+            padd(IQ, "rm", (0, PB[1]))
+            padd(IM1, "W%d" % (t - 1), (0, V), stop=0 if last else None)
+        done = 0
+        for i, (d, lo, hi, hops) in enumerate(mine):
+            ahead = mine[min(i + 1, len(mine) - 1)] if i else mine[0]
+            while done <= max(need(mine[i]), need(ahead)):
+                scan(*parts[done])
+                done += 1
+            send(i)
 
-        arr = [("arr%d" % t, (N - 1) * ne)]
+        if t == 0:
+            act(IQ, IB, ACT.Copy, 0.25); act(IM1, IB, ACT.Copy, -1.0); act(I8, IB, ACT.Copy, 8.0)
+            ts(nb_q, th, BIG, -4 * BIG, ALU.mult, ALU.add)
+            ts(b_r, th, -BIG, BIG / 2, ALU.mult, ALU.add)
+            ts(nb_r, th, BIG, -BIG / 2, ALU.mult, ALU.add)
+            copy(thf, th)
+            for p in (PA, PB):
+                act(home[p], at("rho", p), ACT.Relu, -8 * BIG, nb_q)
+            for p in (PC, PD):
+                tt(at("dif", p), at("rho", p), home[p], ALU.subtract)
+        else:
+            for p in (PC, PD):
+                act(at("rho", p), home[p], ACT.Copy)
+            for p in (PA, PB):
+                act(home[p], at("rb", p), ACT.Relu, -BIG, nb_r)
+            for p in (PC, PD):
+                tt(at("dif", p), home[p], at("u", p), ALU.subtract)
+            padd(I2, "rho", PCD)
+        act(at("rb", PCD), at("dif", PCD), ACT.Relu, 1.0, c716)
+        if t == 0:
+            for p in (PA, PB):
+                tt(at("rm", p), at("ri", p), home[p], ALU.min)
+            padd(IMQ, "rm", (0, PB[1]))
+            copy(("nb16", 0, 256), ("nbi", 0, 256))
+        copy((W, 0, V), ("si", 0, V))
+        padd(IM2, "rb", PCD, stop=1 if last else None)
+        if last:
+            tt(at("dif", H0), bank("P0", H0), at("si", H0), ALU.subtract)
+        for p in (PC, PD):
+            mm(home[p], I8 if last else I1, at("rb", p), True, False, "r%d%d" % (t, p[0]))
+        if t > 0:
+            for p in (PA, PB):
+                tt(at("rb", p), at("rb", p), home[p], ALU.min)
+        if last:
+            tt(at("dif", H1), bank("P1", H1), at("si", H1), ALU.subtract)
+            act(at("po", H0), at("dif", H0), ACT.Identity, 4.0, c35)
+            store("y", T.yp[:, H0[0]:H0[1]], at("po", H0))
+
+        arr = [("arr%d" % t, n_in)]
 
         def lst(i, p):
             return ("nb16", (i * V + p[0]) // 16, (i * V + p[1]) // 16)
 
+        for p in (PC, PD):
+            for i in range(NB):
+                if p == PD and i == 2:
+                    if last:
+                        act(at("rb", PC), home[PC], ACT.Copy)
+                        store("y", T.yr[:, PC[0]:PC[1]], at("rb", PC))
+                    else:
+                        mk_u(PC, home[PC], 8); mk_h(PC)
+                lo = i * NC + p[0] - PC[0]
+                gi = ("G2", lo, lo + p[1] - p[0])
+                gact(gi, (W, 0, WW), lst(i, p), bias=cm35 if (i == 0 and not last) else None,
+                     pre=arr if (i == 0 and p == PC) else ())
+                mm(home[p], I1 if last else IE, gi, False, i == NB - 1, "r%d%d" % (t, p[0]))
         for i in range(NB):
-            gi = ("G2", i * NC, (i + 1) * NC)
-            gact(gi, (W, 0, WW), lst(i, PC), pre=arr if i == 0 else ())
-            mm(bank("R2", PC), I1, gi, False, i == NB - 1, grp)
-            gtt(at("rb", PA), (W, 0, WW), lst(i, PA), at("rb", PA), ALU.add, pre=arr if i == 0 else ())
-            if t == RO - 1 and i == NB - 1:
-                act(at("po", H0), bank("P0", H0), ACT.Copy)
-                store(T.yp[:, H0[0]:H0[1]], at("po", H0))
-                act(at("po", H1), bank("P1", H1), ACT.Copy)
-                store(T.yp[:, H1[0]:H1[1]], at("po", H1))
-                act(at("rb", PC), bank("R2", PC), ACT.Copy)
-                store(T.yr[:, PA[0]:PA[1]], at("rb", PA))
-                store(T.yr[:, PC[0]:PC[1]], at("rb", PC))
-            gtt(at("rb", PB), (W, 0, WW), lst(i, PB), at("rb", PB), ALU.add)
-        if t == RO - 1:
-            store(T.yr[:, PB[0]:PB[1]], at("rb", PB))
+            src = "rm" if (t == 0 and i == 0) else "rb"
+            gtt(at("rb", PA), (W, 0, WW), lst(i, PA), at(src, PA), ALU.add, pre=arr if i == 0 else ())
+            gtt(at("rb", PB), (W, 0, WW), lst(i, PB), at(src, PB), ALU.add)
+        if last:
+            act(("po", H1[0], PB[1]), ("dif", H1[0], PB[1]), ACT.Identity, 4.0, c35)
+            act(at("po", PCD), at("dif", PCD), ACT.Identity, 4.0, c105)
+            store("s", T.yp[:, H1[0]:H1[1]], at("po", H1))
+            act(at("rb", PD), home[PD], ACT.Copy)
+            store("s", T.yr[:, PD[0]:PD[1]], at("rb", PD))
+            store("y", T.yr[:, PA[0]:PA[1]], at("rb", PA))
+            store("y", T.yr[:, PB[0]:PB[1]], at("rb", PB))
 
     emit(ops, queues, T)
-    g.wait_ge(T.sem["snt%d" % (RO - 1)], (N - 1) * ne)
+    g.wait_ge(T.sem["snt%d" % (RO - 1)], n_out)

@@ -1,6 +1,6 @@
 from concourse.mybir import AluOpType as ALU, ActivationFunctionType as ACT
 
-V, G, NB, RO, N = 1024, 384, 4, 3, 8
+V, G, CAP, NB, RO, N = 1024, 384, 96, 4, 3, 8
 SIM_CORES = 256
 WW = V + (N - 1) * G
 PA, PB, PC, PD = (0, 288), (288, 576), (576, 800), (800, 1024)
@@ -10,7 +10,7 @@ BIG = float(2 ** 23)
 
 SCRATCH = {
     "W0": ("sbuf", [128, WW], "float32"), "W1": ("sbuf", [128, WW], "float32"), "W2": ("sbuf", [128, WW], "float32"),
-    "X": ("sbuf", [128, (N - 1) * G], "float32"),
+    "X": ("sbuf", [128, (N - 1) * G + 6 * CAP], "float32"),
     "ri": ("sbuf", [128, V], "int32"), "rb": ("sbuf", [128, V], "float32"), "rm": ("sbuf", [128, V], "float32"),
     "rho": ("sbuf", [128, V], "float32"), "dif": ("sbuf", [128, V], "float32"),
     "si": ("sbuf", [128, V], "int32"), "u": ("sbuf", [128, V], "bfloat16"), "hot": ("sbuf", [128, V], "bfloat16"),
@@ -20,8 +20,8 @@ SCRATCH = {
     "thi": ("sbuf", [128, 8], "int32"), "col": ("sbuf", [128, 48], "float32"),
     "sndi": ("sbuf", [128, 168], "int32"), "snd16": ("sbuf", [128, 168], "uint16"),
     "nbi": ("sbuf", [128, 256], "int32"), "nb16": ("sbuf", [128, 256], "uint16"),
-    "ones": ("sbuf", [128, 128], "bfloat16"), "BD": ("sbuf", [128, 128], "bfloat16"), "IB": ("sbuf", [128, 128], "bfloat16"),
-    "IF": ("sbuf", [128, 1024], "float32"), "zer": ("sbuf", [128, G], "bfloat16"),
+    "ones": ("sbuf", [128, 128], "bfloat16"), "BD": ("sbuf", [128, 128], "bfloat16"),
+    "IF": ("sbuf", [128, 768], "float32"), "zer": ("sbuf", [128, G], "bfloat16"),
     "P0": ("psum", [128, 512], "float32"), "P1": ("psum", [128, 512], "float32"),
     "RC": ("psum", [128, 512], "float32"), "RD": ("psum", [128, 512], "float32"),
     "H1": ("psum", [128, 512], "float32"), "H2": ("psum", [128, 512], "float32"),
@@ -34,12 +34,17 @@ SEMAPHORES = (["c%d" % i for i in range(NCS)] + ["d%d" % i for i in range(NDS)]
 HG = G // 2
 PLAN = {}
 A, B, AB = (0, HG), (HG, G), (0, G)
-ORDER = [("near", 0, A, "m0"), ("near", 0, B, "o0"), ("far", 0, A, "m1"), ("far", 0, B, "o1"), ("far", 1, A, "m0"),
-         ("far", 1, B, "o0"), ("near", 1, A, "m1"), ("dir", 0, A, "f0"), ("near", 1, B, "m0"), ("dir", 0, B, "o1"),
-         ("dir", 1, AB, ""), ("sib", 0, AB, "")]
+HEAD, REST = (0, CAP), (CAP, G)
+PAIRED = ["near", "far", "dir"]
+ORDER = [("near", (0, 1), HEAD, "m0"), ("dir", (0, 1), HEAD, "o0"), ("far", (0, 1), HEAD, "m1"),
+         ("far", (0,), REST, "o1"), ("near", (0,), REST, "m0"), ("far", (1,), REST, "o0"), ("near", (1,), REST, "m1"),
+         ("dir", (0,), REST, ""), ("dir", (1,), REST, ""), ("sib", (0,), AB, "")]
+ORDERS = [ORDER] * RO
+EARLY, LATE = 6, 2
+SPLIT = 512
 
 
-def routes(T, topo):
+def routes(T, topo, order):
     cores = list(T.cores)
     out = {}
     for src in cores:
@@ -54,15 +59,22 @@ def routes(T, topo):
         free = [h for h in topo.cores_of(src) if h not in own and h != src and topo.die(h) == topo.die(src)]
         leave = topo.mask(src, to["dir"][0][2])
         out[src] = []
-        for kind, k, (lo, hi), way in ORDER:
-            _, d, dst = sorted(to[kind])[k]
-            mate = [h for h in range(SIM_CORES) if topo.mates(h, dst) and topo.may_write(h, dst)
-                    and topo.die(h) == topo.die(src)]
-            stops = [src] + [{"o": own, "m": mate, "f": free}[w[0]][int(w[1])] for w in way.split()] + [dst]
-            hops = [(a, b, topo.mask(a, b)) for a, b in zip(stops, stops[1:])]
-            if stops[1] in topo.cores_of(src):
-                hops[0] = (src, stops[1], hops[0][2] & ~leave)
-            out[src].append((d, lo, hi, hops))
+        for kind, ks, (lo, hi), way in order:
+            ends = [sorted(to[kind])[k][1:] for k in ks]
+            first = ends[0][1]
+            if way:
+                mate = [h for h in range(SIM_CORES) if topo.mates(h, first) and topo.may_write(h, first)
+                        and topo.die(h) == topo.die(src)]
+                first = {"o": own, "m": mate, "f": free}[way[0]][int(way[1])]
+            mask = topo.mask(src, first) & (~leave if first in topo.cores_of(src) else leave)
+            if len(ends) > 1:
+                at = PAIRED.index(kind) * len(ends) * (hi - lo)
+                x, w = (N - 1) * G + at, at
+            else:
+                x = (ends[0][0] - 1) * G + lo
+                w = V + x
+            out[src].append({"ds": [d for d, dst in ends], "lo": lo, "hi": hi, "to": first, "mask": mask, "x": x, "w": w,
+                             "on": [dst for d, dst in ends] if way else []})
     return out
 
 
@@ -71,15 +83,8 @@ def bits(m):
 
 
 def relay_jobs(plan, core):
-    return sorted((i, k, d, lo, hi, hops) for src in plan for i, (d, lo, hi, hops) in enumerate(plan[src])
-                  for k in range(1, len(hops)) if hops[k][0] == core)
-
-
-def landing(plan, hops, k, t):
-    if k == len(hops) - 1:
-        return "arr%d" % t
-    slot = [x[5] is hops for x in relay_jobs(plan, hops[k][1])].index(True)
-    return "hop%d_%d" % (slot, t)
+    jobs = [(i, src) for src in plan for i, x in enumerate(plan[src]) if x["on"] and x["to"] == core]
+    return [plan[src][i] for i, src in sorted(jobs)]
 
 
 def emit(ops, queues, T):
@@ -134,39 +139,32 @@ def emit(ops, queues, T):
             queues[o["q"]].wait_ge(T.sem[ev[i][0]], ev[i][1])
 
 
-def helper_program(g, core, T, topo, plan, jobs):
+def helper_program(g, core, T, topo):
     sent = 0
     for t in range(RO):
-        for slot, (i, k, d, lo, hi, hops) in enumerate(jobs):
-            rid, pid = topo.addr(hops[k][1], core)
-            blk = T["W%d" % t][:, V + (d - 1) * G + lo:V + (d - 1) * G + hi]
-            g.wait_ge(T.sem["hop%d_%d" % (slot, t)], bits(hops[k - 1][2]))
-            g.remote_dma(blk, blk, T.sem[landing(plan, hops, k, t)], T.sem.fwd, pid, rid, hops[k][2])
-            sent += bits(hops[k][2])
-    g.wait_ge(T.sem.fwd, sent)
+        W = T["W%d" % t]
+        for slot, x in enumerate(relay_jobs(PLAN[t], core)):
+            g.wait_ge(T.sem["hop%d_%d" % (slot, t)], bits(x["mask"]))
+            n = x["hi"] - x["lo"]
+            for k, (d, dst) in enumerate(zip(x["ds"], x["on"])):
+                rid, pid = topo.addr(dst, core)
+                lo = V + (d - 1) * G + x["lo"]
+                g.remote_dma(W[:, lo:lo + n], W[:, x["w"] + k * n:x["w"] + (k + 1) * n], T.sem["arr%d" % t], T.sem.fwd,
+                             pid, rid, topo.mask(core, dst))
+                sent += bits(topo.mask(core, dst))
+    if sent:
+        g.wait_ge(T.sem.fwd, sent)
 
 
 def rank_program(g, core, T, topo):
     if not PLAN:
-        PLAN.update(routes(T, topo))
-    plan = PLAN
+        PLAN.update({t: routes(T, topo, ORDERS[t]) for t in range(RO)})
     if T.rank_of(core) is None:
-        jobs = relay_jobs(plan, core)
-        if jobs:
-            helper_program(g, core, T, topo, plan, jobs)
+        helper_program(g, core, T, topo)
         return
-    mine = plan[core]
-    n_out = sum(bits(hops[0][2]) for d, lo, hi, hops in mine)
-    n_in = sum(bits(hops[-1][2]) for src in plan for d, lo, hi, hops in plan[src] if hops[-1][1] == core)
-    parts = []
-    for d, lo, hi, hops in mine:
-        part = (d, lo, hi) if d == mine[0][0] else (d, 0, G)
-        if part not in parts:
-            parts.append(part)
-
-    def need(piece):
-        return [k for k, (d, lo, hi) in enumerate(parts) if d == piece[0] and lo <= piece[1] < hi][0]
-
+    n_out = [sum(bits(x["mask"]) for x in PLAN[t][core]) for t in range(RO)]
+    n_in = [sum(bits(x["mask"]) if x["to"] == core else bits(topo.mask(x["to"], core)) if core in x["on"] else 0
+                for src in PLAN[t] for x in PLAN[t][src]) for t in range(RO)]
     v, s_, pe = g.vector, g.scalar, g.tensor
     queues = {"g": g, "v": v, "s": s_, "pe": pe, "y": g.sync}
     ops = []
@@ -226,14 +224,13 @@ def rank_program(g, core, T, topo):
     def bank(b, p, lo=0):
         return (b, lo, lo + p[1] - p[0])
 
-    BD, IB = ("BD", 0, 128), ("IB", 0, 128)
-    I1, I8, IE, I2, IM2, IQ, IMQ, IM1 = [("IF", 128 * k, 128 * k + 128) for k in range(8)]
-    b_r, nb_r, b_q, nb_q, c716, cm35, c35, c105, thf = [("col", 4 * k, 4 * k + 1) for k in range(9)]
+    BD = ("BD", 0, 128)
+    I1, I8, IE, IM8, IM1, IM4 = [("IF", 128 * k, 128 * k + 128) for k in range(6)]
+    b_r, nb_r, b_q, cm716, c716, cm35, c35, c105, thf, chalf = [("col", 4 * k, 4 * k + 1) for k in range(10)]
     th = ("thi", 0, 1)
     H0, H1 = (0, 512), (512, 1024)
     PCD = (PC[0], PD[1])
     home = {PA: bank("UA", PA), PB: bank("UB", PB), PC: bank("RC", PC), PD: bank("RD", PD)}
-    hsum = {PC: bank("H1", PC), PA: bank("H1", PA, PC[1] - PC[0]), PD: bank("H2", PD), PB: bank("H2", PB, PD[1] - PD[0])}
 
     def padd(w, buf, p, start=False, stop=None):
         for k, h in enumerate((H0, H1)):
@@ -248,64 +245,61 @@ def rank_program(g, core, T, topo):
     load("s", at("ri", PD), T.r0[:, PD[0]:PD[1]])
     load("y", ("sndi", 0, 168), T.snd[:])
     load("y", ("nbi", 0, 256), T.nb[:])
-    fill(("ones", 0, 128), 1.0)
     fill(I1, 1.0)
+    fill(("ones", 0, 128), 1.0)
+    fill(cm716, -0.4375)
     fill(("zer", 0, G), 0.0)
-    for c, x in ((c716, 0.4375), (cm35, -3.5), (c35, 3.5), (c105, 10.5)):
+    for c, x in ((chalf, BIG / 2), (c716, 0.4375), (cm35, -3.5), (c35, 3.5), (c105, 10.5)):
         fill(c, x)
-    sel(BD, ("ones", 0, 128), [[-16, 8], [0, 16]], ALU.is_ge, 0, 1)
-    sel(IB, ("ones", 0, 128), [[-1, 128]], ALU.is_equal, 0, 1)
-    sel(BD, BD, [[16, 8], [0, 16]], ALU.is_ge, 15, -1)
     sel(I1, I1, [[-1, 128]], ALU.is_equal, 0, 1)
-    for w, x in ((I2, 2.0), (IM2, -2.0), (IMQ, -0.25), (IE, 0.125)):
-        act(w, IB, ACT.Copy, x)
-    ts(b_q, th, -BIG, 4 * BIG, ALU.mult, ALU.add)
+    sel(BD, ("ones", 0, 128), [[-16, 8], [0, 16]], ALU.is_ge, 0, 1)
+    sel(BD, BD, [[16, 8], [0, 16]], ALU.is_ge, 15, -1)
+    for w, x in ((I8, 8.0), (IE, 0.125), (IM8, -8.0), (IM1, -1.0), (IM4, -4.0)):
+        act(w, I1, ACT.Copy, x)
+    copy(thf, th)
+    act(b_r, th, ACT.Identity, -BIG, chalf)
 
     def mk_u(p, src, unit):
         act(at("u", p), src, ACT.Relu, unit * BIG, b_r if unit == 1 else b_q)
 
     def mk_h(p):
-        mm(hsum[p], BD, at("u", p), True, True)
+        for hb, h in (("H1", H0), ("H2", H1)):
+            lo, hi = max(p[0], h[0]), min(p[1], h[1])
+            if lo < hi:
+                mm((hb, lo - h[0], hi - h[0]), BD, ("u", lo, hi), True, True)
 
-    def mk_U(p):
-        mm(home[p], IB, at("u", p), True, True)
+    def mk_hot():
+        act(at("hot", H0), bank("H1", H0), ACT.Sign)
+        act(at("hot", H1), bank("H2", H1), ACT.Sign)
 
-    def mk_hot(p):
-        act(at("hot", p), hsum[p], ACT.Sign)
+    def u_on_vector(p, src):
+        ts(at("u", p), at(src, p), ap(thf), BIG, ALU.is_ge, ALU.mult, [thf])
 
-    def mk_rho(p):
-        ts(at("rho", p), at("ri", p), 0.125, -0.4375, ALU.mult, ALU.add)
+    def mk_rho(p, src):
+        act(home[p], at(src, p), ACT.Identity, 0.125, cm716)
 
-    def mk_rm(p):
-        tt(at("rm", p), at("rb", p), home[p], ALU.min)
-
-    def s_of_rm(p):
-        ts(at("si", p), at("rm", p), 0.125, -0.4375, ALU.mult, ALU.add)
-
-    def s_of_rho(p, t):
-        tt(at("si", p), at("rho" if t == 0 else "u", p), home[p], ALU.min)
+    def mk_s(p):
+        tt(at("si", p), at("u", p), home[p], ALU.min)
 
     for t in range(RO):
         W = "W%d" % t
         last = t == RO - 1
         if t == 0:
             for p in (PA, PB, PC, PD):
-                mk_rho(p); mk_u(p, at("rho", p), 8)
-                for hb, h in (("H1", H0), ("H2", H1)):
-                    lo, hi = max(p[0], h[0]), min(p[1], h[1])
-                    if lo < hi:
-                        mm((hb, lo - h[0], hi - h[0]), BD, ("u", lo, hi), True, True)
-                mk_U(p)
+                if p in (PA, PB):
+                    u_on_vector(p, "ri")
+                else:
+                    mk_u(p, at("ri", p), 1)
+                mk_rho(p, "ri"); mk_h(p)
+            mk_s(PA); mk_s(PB)
             copy(("snd16", 0, 168), ("sndi", 0, 168))
-            act(("hot", 0, 512), ("H1", 0, 512), ACT.Sign)
-            act(("hot", 512, V), ("H2", 0, 512), ACT.Sign)
-            for p in (PA, PB, PC, PD):
-                s_of_rho(p, t)
+            mk_s(PC); mk_s(PD); mk_hot()
         else:
-            mk_u(PA, at("rb", PA), 1); mk_hot(PC); mk_h(PA); mk_U(PA)
-            ts(at("u", PB), at("rb", PB), ap(thf), BIG, ALU.is_ge, ALU.mult, [thf]); mk_h(PB)
-            mk_u(PD, home[PD], 8); mk_hot(PA); mk_U(PB); mk_h(PD); mk_hot(PB); mk_hot(PD)
-            s_of_rho(PC, t); mk_rm(PA); mk_rm(PB); s_of_rm(PA); s_of_rho(PD, t); s_of_rm(PB)
+            mk_u(PA, at("rb", PA), 1)
+            u_on_vector(PB, "rb"); mk_rho(PA, "rb"); mk_rho(PB, "rb")
+            mk_h(PA); mk_u(PD, home[PD], 8); mk_h(PB); mk_h(PD); mk_hot()
+            for p in (PC, PA, PB, PD):
+                mk_s(p)
 
         def hot_gather(d, lo, hi):
             j = d - 1
@@ -318,100 +312,124 @@ def rank_program(g, core, T, topo):
             op("v", lambda: v.tensor_tensor_scan(ap(m_), ap(h_), ap(z_), ap(prev) if lo else 97.0 * STEP,
                                                  ALU.add, ALU.max), [h_, z_] + ([prev] if lo else []), [m_])
 
-        def send(i, t=t, W=W):
-            d, lo, hi, hops = mine[i]
-            j = d - 1
-            x, w = ("X", j * G + lo, j * G + hi), (W, V + j * G + lo, V + j * G + hi)
-            gtt(x, ("si", 0, V), ("snd16", j * 24 + lo // 16, j * 24 + hi // 16), ("M", j * G + lo, j * G + hi), ALU.min,
-                pre=[("snt%d" % (t - 1), n_out)] if (i == 0 and t > 0) else [])
-            rid, pid = topo.addr(hops[0][1], core)
-            rs = T.sem[landing(plan, hops, 0, t)]
-            op("g", lambda: g.remote_dma(ap(w), ap(x), rs, T.sem["snt%d" % t], pid, rid, hops[0][2]),
+        def send(p, t=t, W=W):
+            j, lo, hi = p["ds"][0] - 1, max(p["lo"], CAP), p["hi"]
+            n = (hi - p["lo"]) * len(p["ds"])
+            x, w = ("X", p["x"], p["x"] + n), (W, p["w"], p["w"] + n)
+            if hi > CAP:
+                gtt(("X", j * G + lo, j * G + hi), ("si", 0, V), ("snd16", j * 24 + lo // 16, j * 24 + hi // 16),
+                    ("M", j * G + lo, j * G + hi), ALU.min)
+            rid, pid = topo.addr(p["to"], core)
+            slot = [y is p for y in relay_jobs(PLAN[t], p["to"])].index(True) if p["on"] else None
+            rs = T.sem["hop%d_%d" % (slot, t) if p["on"] else "arr%d" % t]
+            op("g", lambda: g.remote_dma(ap(w), ap(x), rs, T.sem["snt%d" % t], pid, rid, p["mask"]),
                [x], [], remote=True)
 
-        for part in parts:
-            hot_gather(*part)
-        if t == 0:
-            padd(I2, "rho", (0, V), start=True)
+        def head(d, on_vector=False, pre=()):
+            lo = [p["x"] + p["ds"].index(d) * CAP for p in mine if d in p["ds"] and p["lo"] == 0][0]
+            x, lst = ("X", lo, lo + CAP), ("snd16", (d - 1) * 24, (d - 1) * 24 + CAP // 16)
+            if on_vector:
+                op("v", lambda: v.tensor_copy(ap(x), T.si[:, 0:V].indirect(ap(lst))), [("si", 0, V), lst], [x], pre=pre)
+            else:
+                gact(x, ("si", 0, V), lst, pre=pre)
+
+        mine = PLAN[t][core]
+        early = []
+        for d in [d for p in mine for d in p["ds"]]:
+            if d not in early and len(early) < EARLY:
+                early.append(d)
+        parts = []
+        for p in mine:
+            d, hi = p["ds"][0], p["hi"]
+            if hi > CAP and not [x for x in parts if x[0] == d and x[2] >= hi]:
+                start = max([0] + [x[2] for x in parts if x[0] == d])
+                parts.append((d, start, G if parts else hi))
+
+        def need(p, parts=parts):
+            return max([-1] + [k for k, x in enumerate(parts) if x[0] == p["ds"][0] and CAP < p["hi"] > x[1]])
+
+        free = [("snt%d" % (t - 1), n_out[t - 1])] if t > 0 else []
+        for d in early:
+            head(d, True, free if d == early[0] else [])
+        wait = free
+        late = [d for p in mine for d in p["ds"] if p["lo"] == 0 and d not in early]
+        for k, (d, lo, hi) in enumerate(parts):
+            hot_gather(d, lo, hi)
+            while late and (k + 1 == LATE and len(late) > 1 or late[0] == d):
+                head(late.pop(0), False, wait)
+                wait = []
+        if t > 0:
+            padd(IM8, "rm", PCD)
+            padd(IM1, "rm", (0, PB[1]))
+            padd(I1, "rb", (0, PB[1]))
+            padd(IM4, "W%d" % (t - 1), (0, V), stop=0 if last else None)
         else:
-            padd(IQ, "rm", (0, PB[1]))
-            padd(IM1, "W%d" % (t - 1), (0, V), stop=0 if last else None)
+            ts(nb_r, th, BIG, -BIG / 2, ALU.mult, ALU.add)
+            ts(b_q, th, -BIG, 4 * BIG, ALU.mult, ALU.add)
         done = 0
-        for i, (d, lo, hi, hops) in enumerate(mine):
-            ahead = mine[min(i + 1, len(mine) - 1)] if i else mine[0]
-            while done <= max(need(mine[i]), need(ahead)):
+        for i, p in enumerate(mine):
+            ahead = mine[min(i + 1, len(mine) - 1)] if done > 1 else p
+            while done <= max(need(p), need(ahead)):
                 scan(*parts[done])
                 done += 1
-            send(i)
+            send(p)
 
-        if t == 0:
-            act(IQ, IB, ACT.Copy, 0.25); act(IM1, IB, ACT.Copy, -1.0); act(I8, IB, ACT.Copy, 8.0)
-            ts(nb_q, th, BIG, -4 * BIG, ALU.mult, ALU.add)
-            ts(b_r, th, -BIG, BIG / 2, ALU.mult, ALU.add)
-            ts(nb_r, th, BIG, -BIG / 2, ALU.mult, ALU.add)
-            copy(thf, th)
-            for p in (PA, PB):
-                act(home[p], at("rho", p), ACT.Relu, -8 * BIG, nb_q)
-            for p in (PC, PD):
-                tt(at("dif", p), at("rho", p), home[p], ALU.subtract)
-        else:
-            for p in (PC, PD):
-                act(at("rho", p), home[p], ACT.Copy)
-            for p in (PA, PB):
-                act(home[p], at("rb", p), ACT.Relu, -BIG, nb_r)
-            for p in (PC, PD):
-                tt(at("dif", p), home[p], at("u", p), ALU.subtract)
-            padd(I2, "rho", PCD)
-        act(at("rb", PCD), at("dif", PCD), ACT.Relu, 1.0, c716)
-        if t == 0:
-            for p in (PA, PB):
-                tt(at("rm", p), at("ri", p), home[p], ALU.min)
-            padd(IMQ, "rm", (0, PB[1]))
-            copy(("nb16", 0, 256), ("nbi", 0, 256))
-        copy((W, 0, V), ("si", 0, V))
-        padd(IM2, "rb", PCD, stop=1 if last else None)
-        if last:
-            tt(at("dif", H0), bank("P0", H0), at("si", H0), ALU.subtract)
+        for p in (PC, PD) if t else (PC, PD, PA, PB):
+            act(at("rho", p), home[p], ACT.Copy)
+        padd(I8, "rho", PCD if t else (0, V), start=t == 0, stop=1 if last else None)
+        for p in (PA, PB):
+            act(home[p], at("rb" if t else "ri", p), ACT.Relu, -BIG, nb_r)
         for p in (PC, PD):
-            mm(home[p], I8 if last else I1, at("rb", p), True, False, "r%d%d" % (t, p[0]))
-        if t > 0:
-            for p in (PA, PB):
-                tt(at("rb", p), at("rb", p), home[p], ALU.min)
+            tt(at("dif", p), home[p], at("u", p), ALU.subtract)
         if last:
-            tt(at("dif", H1), bank("P1", H1), at("si", H1), ALU.subtract)
-            act(at("po", H0), at("dif", H0), ACT.Identity, 4.0, c35)
-            store("y", T.yp[:, H0[0]:H0[1]], at("po", H0))
+            act(at("rm", PCD), at("dif", PCD), ACT.Relu, 8.0, c35)
+        else:
+            act(at("rm", PCD), at("dif", PCD), ACT.Relu, 1.0, c716)
+        for p in (PA, PB):
+            tt(at("rm", p), at("rb" if t else "ri", p), home[p], ALU.min)
+        for p in (PC, PD):
+            mm(home[p], I1, at("rm", p), True, False, "r%d%d" % (t, p[0]))
+        copy((W, 0, SPLIT), ("si", 0, SPLIT))
+        act((W, SPLIT, V), ("si", SPLIT, V), ACT.Copy)
+        if t == 0:
+            copy(("nb16", 0, 256), ("nbi", 0, 256))
+        if last:
+            act(("dif", 0, PB[1]), ("si", 0, PB[1]), ACT.Identity, -4.0, c35)
+            act(at("dif", PCD), at("si", PCD), ACT.Identity, -4.0, c105)
+            tt(bank("P0", H0), bank("P0", H0), at("rm", H0), ALU.subtract)
+            tt(bank("P1", H1), bank("P1", H1), at("rm", H1), ALU.subtract)
+            for k, h in enumerate((H0, H1)):
+                tt(at("po", h), bank("P%d" % k, h), at("dif", h), ALU.add)
+                store("y", T.yp[:, h[0]:h[1]], at("po", h))
 
-        arr = [("arr%d" % t, n_in)]
+        arr = [("arr%d" % t, n_in[t])]
 
         def lst(i, p):
             return ("nb16", (i * V + p[0]) // 16, (i * V + p[1]) // 16)
 
         for p in (PC, PD):
             for i in range(NB):
-                if p == PD and i == 2:
-                    if last:
-                        act(at("rb", PC), home[PC], ACT.Copy)
-                        store("y", T.yr[:, PC[0]:PC[1]], at("rb", PC))
-                    else:
-                        mk_u(PC, home[PC], 8); mk_h(PC)
                 lo = i * NC + p[0] - PC[0]
                 gi = ("G2", lo, lo + p[1] - p[0])
                 gact(gi, (W, 0, WW), lst(i, p), bias=cm35 if (i == 0 and not last) else None,
                      pre=arr if (i == 0 and p == PC) else ())
-                mm(home[p], I1 if last else IE, gi, False, i == NB - 1, "r%d%d" % (t, p[0]))
+                n_mm = NB - 1 if (last and p == PD) else NB
+                if i < n_mm:
+                    mm(home[p], I1 if last else IE, gi, False, i == n_mm - 1, "r%d%d" % (t, p[0]))
+        if last:
+            act(at("rb", PC), home[PC], ACT.Copy)
+            store("y", T.yr[:, PC[0]:PC[1]], at("rb", PC))
+        else:
+            mk_u(PC, home[PC], 8); mk_h(PC)
         for i in range(NB):
-            src = "rm" if (t == 0 and i == 0) else "rb"
+            src = "rm" if i == 0 else "rb"
             gtt(at("rb", PA), (W, 0, WW), lst(i, PA), at(src, PA), ALU.add, pre=arr if i == 0 else ())
             gtt(at("rb", PB), (W, 0, WW), lst(i, PB), at(src, PB), ALU.add)
         if last:
-            act(("po", H1[0], PB[1]), ("dif", H1[0], PB[1]), ACT.Identity, 4.0, c35)
-            act(at("po", PCD), at("dif", PCD), ACT.Identity, 4.0, c105)
-            store("s", T.yp[:, H1[0]:H1[1]], at("po", H1))
-            act(at("rb", PD), home[PD], ACT.Copy)
+            tt(at("rb", PD), home[PD], gi, ALU.add)
             store("s", T.yr[:, PD[0]:PD[1]], at("rb", PD))
             store("y", T.yr[:, PA[0]:PA[1]], at("rb", PA))
             store("y", T.yr[:, PB[0]:PB[1]], at("rb", PB))
 
     emit(ops, queues, T)
-    g.wait_ge(T.sem["snt%d" % (RO - 1)], n_out)
+    g.wait_ge(T.sem["snt%d" % (RO - 1)], n_out[RO - 1])

from concourse.mybir import AluOpType as ALU, ActivationFunctionType as ACT

V, G, CAP, NB, RO, N = 1024, 384, 96, 4, 3, 8
SIM_CORES = 256
WW = V + (N - 1) * G
PA, PB, PC, PD = (0, 288), (288, 576), (576, 800), (800, 1024)
NC = PD[1] - PC[0]
STEP = float(2 ** 19)
BIG = float(2 ** 23)

SCRATCH = {
    "W0": ("sbuf", [128, WW], "float32"), "W1": ("sbuf", [128, WW], "float32"), "W2": ("sbuf", [128, WW], "float32"),
    "X": ("sbuf", [128, (N - 1) * G + 6 * CAP], "float32"),
    "ri": ("sbuf", [128, V], "int32"), "rb": ("sbuf", [128, V], "float32"), "rm": ("sbuf", [128, V], "float32"),
    "rho": ("sbuf", [128, V], "float32"), "dif": ("sbuf", [128, V], "float32"),
    "si": ("sbuf", [128, V], "int32"), "u": ("sbuf", [128, V], "bfloat16"), "hot": ("sbuf", [128, V], "bfloat16"),
    "po": ("sbuf", [128, V], "float32"),
    "Hg": ("sbuf", [128, (N - 1) * G], "bfloat16"), "M": ("sbuf", [128, (N - 1) * G], "bfloat16"),
    "G2": ("sbuf", [128, NB * NC], "float32"),
    "thi": ("sbuf", [128, 8], "int32"), "col": ("sbuf", [128, 48], "float32"),
    "sndi": ("sbuf", [128, 168], "int32"), "snd16": ("sbuf", [128, 168], "uint16"),
    "nbi": ("sbuf", [128, 256], "int32"), "nb16": ("sbuf", [128, 256], "uint16"),
    "ones": ("sbuf", [128, 128], "bfloat16"), "BD": ("sbuf", [128, 128], "bfloat16"),
    "IF": ("sbuf", [128, 768], "float32"), "zer": ("sbuf", [128, G], "bfloat16"),
    "P0": ("psum", [128, 512], "float32"), "P1": ("psum", [128, 512], "float32"),
    "RC": ("psum", [128, 512], "float32"), "RD": ("psum", [128, 512], "float32"),
    "H1": ("psum", [128, 512], "float32"), "H2": ("psum", [128, 512], "float32"),
    "UA": ("psum", [128, 512], "float32"), "UB": ("psum", [128, 512], "float32"),
}
NCS, NDS = 90, 14
SEMAPHORES = (["c%d" % i for i in range(NCS)] + ["d%d" % i for i in range(NDS)]
              + ["arr%d" % t for t in range(RO)] + ["snt%d" % t for t in range(RO)]
              + ["hop%d_%d" % (j, t) for j in range(6) for t in range(RO)] + ["fwd"])
HG = G // 2
PLAN = {}
A, B, AB = (0, HG), (HG, G), (0, G)
HEAD, REST = (0, CAP), (CAP, G)
PAIRED = ["near", "far", "dir"]
ORDER = [("near", (0, 1), HEAD, "m0"), ("dir", (0, 1), HEAD, "o0"), ("far", (0, 1), HEAD, "m1"),
         ("far", (0,), REST, "o1"), ("near", (0,), REST, "m0"), ("far", (1,), REST, "o0"), ("near", (1,), REST, "m1"),
         ("dir", (0,), REST, ""), ("dir", (1,), REST, ""), ("sib", (0,), AB, "")]
ORDERS = [ORDER] * RO
EARLY, LATE = 6, 2
SPLIT = 512


def routes(T, topo, order):
    cores = list(T.cores)
    out = {}
    for src in cores:
        to = {"sib": [], "dir": [], "near": [], "far": []}
        for d in range(1, N):
            dst = cores[(cores.index(src) + d) % N]
            kind = ("sib" if dst in topo.cores_of(src) else "dir" if topo.may_write(src, dst)
                    else "near" if topo.host(dst) == topo.host(src) else "far")
            to[kind].append((topo.die(dst) == topo.die(src), d, dst))
        other = to["near"][0][2]
        own = [h for h in topo.cores_of(src) if topo.may_write(h, other) and topo.die(h) == topo.die(src)]
        free = [h for h in topo.cores_of(src) if h not in own and h != src and topo.die(h) == topo.die(src)]
        leave = topo.mask(src, to["dir"][0][2])
        out[src] = []
        for kind, ks, (lo, hi), way in order:
            ends = [sorted(to[kind])[k][1:] for k in ks]
            first = ends[0][1]
            if way:
                mate = [h for h in range(SIM_CORES) if topo.mates(h, first) and topo.may_write(h, first)
                        and topo.die(h) == topo.die(src)]
                first = {"o": own, "m": mate, "f": free}[way[0]][int(way[1])]
            mask = topo.mask(src, first) & (~leave if first in topo.cores_of(src) else leave)
            if len(ends) > 1:
                at = PAIRED.index(kind) * len(ends) * (hi - lo)
                x, w = (N - 1) * G + at, at
            else:
                x = (ends[0][0] - 1) * G + lo
                w = V + x
            out[src].append({"ds": [d for d, dst in ends], "lo": lo, "hi": hi, "to": first, "mask": mask, "x": x, "w": w,
                             "on": [dst for d, dst in ends] if way else []})
    return out


def bits(m):
    return bin(m).count("1")


def relay_jobs(plan, core):
    jobs = [(i, src) for src in plan for i, x in enumerate(plan[src]) if x["on"] and x["to"] == core]
    return [plan[src][i] for i, src in sorted(jobs)]


def emit(ops, queues, T):
    n = len(ops)
    known = {q: set() for q in queues}
    closure, deps, before = [None] * n, [None] * n, [None] * n
    for i, o in enumerate(ops):
        q = o["q"]
        need = []
        for j in range(i - 1, -1, -1):
            p = ops[j]
            if j in known[q] or p["remote"]:
                continue
            hit = False
            for (b, lo, hi, w) in o["acc"]:
                for (b2, lo2, hi2, w2) in p["acc"]:
                    if b != b2:
                        continue
                    if SCRATCH[b][0] == "psum":
                        if o["grp"] is not None and o["grp"] == p["grp"]:
                            continue
                        if w or w2 or q != p["q"]:
                            hit = True
                    elif (w or w2) and lo < hi2 and lo2 < hi:
                        hit = True
            if hit:
                need.append(j)
                known[q] |= closure[j]
        deps[i] = need
        before[i] = set(known[q])
        closure[i] = before[i] | {i}
    waited = set(j for d in deps for j in d) | set(i for i in range(n) if ops[i]["final"])
    last = {}
    ev = {}
    for i, o in enumerate(ops):
        eng = queues[o["q"]]
        for j in deps[i]:
            eng.wait_ge(T.sem[ev[j][0]], ev[j][1])
        for (s, c) in o["pre"]:
            eng.wait_ge(T.sem[s], c)
        ins = o["fn"]()
        if i in waited:
            pool = ["d%d" % k for k in range(NDS)] if o["dma"] else ["c%d" % k for k in range(NCS)]
            s = [x for x in pool if x not in last or last[x][0] in before[i]][0]
            step = 16 if o["dma"] else 1
            c = (last[s][1] if s in last else 0) + step
            last[s] = (i, c)
            ev[i] = (s, c)
            ins.then_inc(T.sem[s], step)
    for i, o in enumerate(ops):
        if o["final"]:
            queues[o["q"]].wait_ge(T.sem[ev[i][0]], ev[i][1])


def helper_program(g, core, T, topo):
    sent = 0
    for t in range(RO):
        W = T["W%d" % t]
        for slot, x in enumerate(relay_jobs(PLAN[t], core)):
            g.wait_ge(T.sem["hop%d_%d" % (slot, t)], bits(x["mask"]))
            n = x["hi"] - x["lo"]
            for k, (d, dst) in enumerate(zip(x["ds"], x["on"])):
                rid, pid = topo.addr(dst, core)
                lo = V + (d - 1) * G + x["lo"]
                g.remote_dma(W[:, lo:lo + n], W[:, x["w"] + k * n:x["w"] + (k + 1) * n], T.sem["arr%d" % t], T.sem.fwd,
                             pid, rid, topo.mask(core, dst))
                sent += bits(topo.mask(core, dst))
    if sent:
        g.wait_ge(T.sem.fwd, sent)


def rank_program(g, core, T, topo):
    if not PLAN:
        PLAN.update({t: routes(T, topo, ORDERS[t]) for t in range(RO)})
    if T.rank_of(core) is None:
        helper_program(g, core, T, topo)
        return
    n_out = [sum(bits(x["mask"]) for x in PLAN[t][core]) for t in range(RO)]
    n_in = [sum(bits(x["mask"]) if x["to"] == core else bits(topo.mask(x["to"], core)) if core in x["on"] else 0
                for src in PLAN[t] for x in PLAN[t][src]) for t in range(RO)]
    v, s_, pe = g.vector, g.scalar, g.tensor
    queues = {"g": g, "v": v, "s": s_, "pe": pe, "y": g.sync}
    ops = []

    def op(q, fn, reads, writes, grp=None, pre=(), dma=False, final=False, remote=False):
        acc = [(b, lo, hi, False) for (b, lo, hi) in reads] + [(b, lo, hi, True) for (b, lo, hi) in writes]
        ops.append({"q": q, "fn": fn, "acc": acc, "grp": grp, "pre": list(pre), "dma": dma, "final": final,
                    "remote": remote})

    def ap(x):
        return T[x[0]][:, x[1]:x[2]]

    def load(q, dst, src):
        op(q, lambda: queues[q].dma_start(ap(dst), src), [], [dst], dma=True)

    def store(q, dst, src):
        op(q, lambda: queues[q].dma_start(dst, ap(src)), [src], [], dma=True, final=True)

    def copy(out, in_):
        op("v", lambda: v.tensor_copy(ap(out), ap(in_)), [in_], [out])

    def fill(out, c):
        op("v", lambda: v.memset(ap(out), c), [], [out])

    def ts(out, in_, a, b, o0, o1, cols=()):
        op("v", lambda: v.tensor_scalar(ap(out), ap(in_), a, b, o0, o1), [in_] + list(cols), [out])

    def tt(out, a, b, o):
        op("v", lambda: v.tensor_tensor(ap(out), ap(a), ap(b), o), [a, b], [out])

    def gtt(out, win, lst, b, o, pre=()):
        op("v", lambda: v.tensor_tensor(ap(out), ap(win).indirect(ap(lst)), ap(b), o), [win, lst, b], [out], pre=pre)

    def act(out, in_, f, scale=1.0, bias=None):
        if bias is None:
            op("s", lambda: s_.activation(ap(out), ap(in_), f, scale=scale), [in_], [out])
        else:
            op("s", lambda: s_.activation(ap(out), ap(in_), f, bias=ap(bias), scale=scale), [in_, bias], [out])

    def gact(out, win, lst, scale=1.0, bias=None, pre=()):
        if bias is None:
            op("s", lambda: s_.activation(ap(out), ap(win).indirect(ap(lst)), ACT.Copy, scale=scale),
               [win, lst], [out], pre=pre)
        else:
            op("s", lambda: s_.activation(ap(out), ap(win).indirect(ap(lst)), ACT.Identity, bias=ap(bias), scale=scale),
               [win, lst, bias], [out], pre=pre)

    def mm(out, w, x, start, stop, grp=None):
        op("pe", lambda: pe.matmul(ap(out), ap(w), ap(x), start, stop), [w, x], [out], grp=grp)

    def sel(out, in_, pat, cmp, base, cm):
        op("g", lambda: g.affine_select(ap(out), ap(in_), pat, cmp, 0.0, base, cm), [in_], [out])

    def at(b, p):
        return (b, p[0], p[1])

    def bank(b, p, lo=0):
        return (b, lo, lo + p[1] - p[0])

    BD = ("BD", 0, 128)
    I1, I8, IE, IM8, IM1, IM4 = [("IF", 128 * k, 128 * k + 128) for k in range(6)]
    b_r, nb_r, b_q, cm716, c716, cm35, c35, c105, thf, chalf = [("col", 4 * k, 4 * k + 1) for k in range(10)]
    th = ("thi", 0, 1)
    H0, H1 = (0, 512), (512, 1024)
    PCD = (PC[0], PD[1])
    home = {PA: bank("UA", PA), PB: bank("UB", PB), PC: bank("RC", PC), PD: bank("RD", PD)}

    def padd(w, buf, p, start=False, stop=None):
        for k, h in enumerate((H0, H1)):
            lo, hi = max(p[0], h[0]), min(p[1], h[1])
            if lo < hi:
                mm(("P%d" % k, lo - h[0], hi - h[0]), w, (buf, lo, hi), start, stop == k, "p%d" % k)

    load("s", th, T.th[:])
    load("y", at("ri", PA), T.r0[:, PA[0]:PA[1]])
    load("s", at("ri", PB), T.r0[:, PB[0]:PB[1]])
    load("y", at("ri", PC), T.r0[:, PC[0]:PC[1]])
    load("s", at("ri", PD), T.r0[:, PD[0]:PD[1]])
    load("y", ("sndi", 0, 168), T.snd[:])
    load("y", ("nbi", 0, 256), T.nb[:])
    fill(I1, 1.0)
    fill(("ones", 0, 128), 1.0)
    fill(cm716, -0.4375)
    fill(("zer", 0, G), 0.0)
    for c, x in ((chalf, BIG / 2), (c716, 0.4375), (cm35, -3.5), (c35, 3.5), (c105, 10.5)):
        fill(c, x)
    sel(I1, I1, [[-1, 128]], ALU.is_equal, 0, 1)
    sel(BD, ("ones", 0, 128), [[-16, 8], [0, 16]], ALU.is_ge, 0, 1)
    sel(BD, BD, [[16, 8], [0, 16]], ALU.is_ge, 15, -1)
    for w, x in ((I8, 8.0), (IE, 0.125), (IM8, -8.0), (IM1, -1.0), (IM4, -4.0)):
        act(w, I1, ACT.Copy, x)
    copy(thf, th)
    act(b_r, th, ACT.Identity, -BIG, chalf)

    def mk_u(p, src, unit):
        act(at("u", p), src, ACT.Relu, unit * BIG, b_r if unit == 1 else b_q)

    def mk_h(p):
        for hb, h in (("H1", H0), ("H2", H1)):
            lo, hi = max(p[0], h[0]), min(p[1], h[1])
            if lo < hi:
                mm((hb, lo - h[0], hi - h[0]), BD, ("u", lo, hi), True, True)

    def mk_hot():
        act(at("hot", H0), bank("H1", H0), ACT.Sign)
        act(at("hot", H1), bank("H2", H1), ACT.Sign)

    def u_on_vector(p, src):
        ts(at("u", p), at(src, p), ap(thf), BIG, ALU.is_ge, ALU.mult, [thf])

    def mk_rho(p, src):
        act(home[p], at(src, p), ACT.Identity, 0.125, cm716)

    def mk_s(p):
        tt(at("si", p), at("u", p), home[p], ALU.min)

    for t in range(RO):
        W = "W%d" % t
        last = t == RO - 1
        if t == 0:
            for p in (PA, PB, PC, PD):
                if p in (PA, PB):
                    u_on_vector(p, "ri")
                else:
                    mk_u(p, at("ri", p), 1)
                mk_rho(p, "ri"); mk_h(p)
            mk_s(PA); mk_s(PB)
            copy(("snd16", 0, 168), ("sndi", 0, 168))
            mk_s(PC); mk_s(PD); mk_hot()
        else:
            mk_u(PA, at("rb", PA), 1)
            u_on_vector(PB, "rb"); mk_rho(PA, "rb"); mk_rho(PB, "rb")
            mk_h(PA); mk_u(PD, home[PD], 8); mk_h(PB); mk_h(PD); mk_hot()
            for p in (PC, PA, PB, PD):
                mk_s(p)

        def hot_gather(d, lo, hi):
            j = d - 1
            gact(("Hg", j * G + lo, j * G + hi), ("hot", 0, V), ("snd16", j * 24 + lo // 16, j * 24 + hi // 16), -STEP)

        def scan(d, lo, hi):
            j = d - 1
            m_, h_, z_ = ("M", j * G + lo, j * G + hi), ("Hg", j * G + lo, j * G + hi), ("zer", lo, hi)
            prev = ("M", j * G + lo - 1, j * G + lo)
            op("v", lambda: v.tensor_tensor_scan(ap(m_), ap(h_), ap(z_), ap(prev) if lo else 97.0 * STEP,
                                                 ALU.add, ALU.max), [h_, z_] + ([prev] if lo else []), [m_])

        def send(p, t=t, W=W):
            j, lo, hi = p["ds"][0] - 1, max(p["lo"], CAP), p["hi"]
            n = (hi - p["lo"]) * len(p["ds"])
            x, w = ("X", p["x"], p["x"] + n), (W, p["w"], p["w"] + n)
            if hi > CAP:
                gtt(("X", j * G + lo, j * G + hi), ("si", 0, V), ("snd16", j * 24 + lo // 16, j * 24 + hi // 16),
                    ("M", j * G + lo, j * G + hi), ALU.min)
            rid, pid = topo.addr(p["to"], core)
            slot = [y is p for y in relay_jobs(PLAN[t], p["to"])].index(True) if p["on"] else None
            rs = T.sem["hop%d_%d" % (slot, t) if p["on"] else "arr%d" % t]
            op("g", lambda: g.remote_dma(ap(w), ap(x), rs, T.sem["snt%d" % t], pid, rid, p["mask"]),
               [x], [], remote=True)

        def head(d, on_vector=False, pre=()):
            lo = [p["x"] + p["ds"].index(d) * CAP for p in mine if d in p["ds"] and p["lo"] == 0][0]
            x, lst = ("X", lo, lo + CAP), ("snd16", (d - 1) * 24, (d - 1) * 24 + CAP // 16)
            if on_vector:
                op("v", lambda: v.tensor_copy(ap(x), T.si[:, 0:V].indirect(ap(lst))), [("si", 0, V), lst], [x], pre=pre)
            else:
                gact(x, ("si", 0, V), lst, pre=pre)

        mine = PLAN[t][core]
        early = []
        for d in [d for p in mine for d in p["ds"]]:
            if d not in early and len(early) < EARLY:
                early.append(d)
        parts = []
        for p in mine:
            d, hi = p["ds"][0], p["hi"]
            if hi > CAP and not [x for x in parts if x[0] == d and x[2] >= hi]:
                start = max([0] + [x[2] for x in parts if x[0] == d])
                parts.append((d, start, G if parts else hi))

        def need(p, parts=parts):
            return max([-1] + [k for k, x in enumerate(parts) if x[0] == p["ds"][0] and CAP < p["hi"] > x[1]])

        free = [("snt%d" % (t - 1), n_out[t - 1])] if t > 0 else []
        for d in early:
            head(d, True, free if d == early[0] else [])
        wait = free
        late = [d for p in mine for d in p["ds"] if p["lo"] == 0 and d not in early]
        for k, (d, lo, hi) in enumerate(parts):
            hot_gather(d, lo, hi)
            while late and (k + 1 == LATE and len(late) > 1 or late[0] == d):
                head(late.pop(0), False, wait)
                wait = []
        if t > 0:
            padd(IM8, "rm", PCD)
            padd(IM1, "rm", (0, PB[1]))
            padd(I1, "rb", (0, PB[1]))
            padd(IM4, "W%d" % (t - 1), (0, V), stop=0 if last else None)
        else:
            ts(nb_r, th, BIG, -BIG / 2, ALU.mult, ALU.add)
            ts(b_q, th, -BIG, 4 * BIG, ALU.mult, ALU.add)
        done = 0
        for i, p in enumerate(mine):
            ahead = mine[min(i + 1, len(mine) - 1)] if done > 1 else p
            while done <= max(need(p), need(ahead)):
                scan(*parts[done])
                done += 1
            send(p)

        for p in (PC, PD) if t else (PC, PD, PA, PB):
            act(at("rho", p), home[p], ACT.Copy)
        padd(I8, "rho", PCD if t else (0, V), start=t == 0, stop=1 if last else None)
        for p in (PA, PB):
            act(home[p], at("rb" if t else "ri", p), ACT.Relu, -BIG, nb_r)
        for p in (PC, PD):
            tt(at("dif", p), home[p], at("u", p), ALU.subtract)
        if last:
            act(at("rm", PCD), at("dif", PCD), ACT.Relu, 8.0, c35)
        else:
            act(at("rm", PCD), at("dif", PCD), ACT.Relu, 1.0, c716)
        for p in (PA, PB):
            tt(at("rm", p), at("rb" if t else "ri", p), home[p], ALU.min)
        for p in (PC, PD):
            mm(home[p], I1, at("rm", p), True, False, "r%d%d" % (t, p[0]))
        copy((W, 0, SPLIT), ("si", 0, SPLIT))
        act((W, SPLIT, V), ("si", SPLIT, V), ACT.Copy)
        if t == 0:
            copy(("nb16", 0, 256), ("nbi", 0, 256))
        if last:
            act(("dif", 0, PB[1]), ("si", 0, PB[1]), ACT.Identity, -4.0, c35)
            act(at("dif", PCD), at("si", PCD), ACT.Identity, -4.0, c105)
            tt(bank("P0", H0), bank("P0", H0), at("rm", H0), ALU.subtract)
            tt(bank("P1", H1), bank("P1", H1), at("rm", H1), ALU.subtract)
            for k, h in enumerate((H0, H1)):
                tt(at("po", h), bank("P%d" % k, h), at("dif", h), ALU.add)
                store("y", T.yp[:, h[0]:h[1]], at("po", h))

        arr = [("arr%d" % t, n_in[t])]

        def lst(i, p):
            return ("nb16", (i * V + p[0]) // 16, (i * V + p[1]) // 16)

        for p in (PC, PD):
            for i in range(NB):
                lo = i * NC + p[0] - PC[0]
                gi = ("G2", lo, lo + p[1] - p[0])
                gact(gi, (W, 0, WW), lst(i, p), bias=cm35 if (i == 0 and not last) else None,
                     pre=arr if (i == 0 and p == PC) else ())
                n_mm = NB - 1 if (last and p == PD) else NB
                if i < n_mm:
                    mm(home[p], I1 if last else IE, gi, False, i == n_mm - 1, "r%d%d" % (t, p[0]))
        if last:
            act(at("rb", PC), home[PC], ACT.Copy)
            store("y", T.yr[:, PC[0]:PC[1]], at("rb", PC))
        else:
            mk_u(PC, home[PC], 8); mk_h(PC)
        for i in range(NB):
            src = "rm" if i == 0 else "rb"
            gtt(at("rb", PA), (W, 0, WW), lst(i, PA), at(src, PA), ALU.add, pre=arr if i == 0 else ())
            gtt(at("rb", PB), (W, 0, WW), lst(i, PB), at(src, PB), ALU.add)
        if last:
            tt(at("rb", PD), home[PD], gi, ALU.add)
            store("s", T.yr[:, PD[0]:PD[1]], at("rb", PD))
            store("y", T.yr[:, PA[0]:PA[1]], at("rb", PA))
            store("y", T.yr[:, PB[0]:PB[1]], at("rb", PB))

    emit(ops, queues, T)
    g.wait_ge(T.sem["snt%d" % (RO - 1)], n_out[RO - 1])
